import numpy as np
import ml_dtypes


def mxq(x, axis, fmt="e4m3"):
    dtype, down = {"e4m3": (ml_dtypes.float8_e4m3fn, 7), "e5m2": (ml_dtypes.float8_e5m2, 14)}[fmt]
    v = np.moveaxis(np.asarray(x, np.float32).astype(ml_dtypes.bfloat16).astype(np.float64), axis, -1)
    blocks = v.reshape(v.shape[:-1] + (-1, 32))
    amax = np.abs(blocks).max(-1, keepdims=True)
    byte = np.maximum(np.where(amax > 0, np.frexp(amax)[1] - 1 + 127, 0) - down, 1)
    scale = np.exp2(byte - 127.0)
    codes = (blocks / scale).astype(np.float32).astype(dtype).astype(np.float64)
    return np.moveaxis((codes * scale).reshape(v.shape), -1, axis)


WIDE = False


def mx_kscale(k):
    if not WIDE:
        return np.ones(k)
    levels = np.array([10, -10, 5, -5, 0])
    if k % 512:
        return np.exp2(np.random.permutation(np.resize(levels, k // 32))).repeat(32)
    a = np.empty((k // 512, 16))
    for p in range(k // 512):
        a[p, :8] = np.random.permutation(np.resize(levels, 8))
        for g in range(8):
            far = levels[np.abs(levels - a[p, g]) >= 10]
            a[p, g + 8] = far[np.random.randint(len(far))]
    return np.exp2(a.ravel()).repeat(32)


BF16 = ml_dtypes.bfloat16


def bf(x):
    return np.asarray(x, np.float32).astype(BF16)


def f64(x):
    return np.asarray(x).astype(np.float64)


E2M1 = np.array([0.0, 0.5, 1.0, 1.5, 2.0, 3.0, 4.0, 6.0, -0.0, -0.5, -1.0, -1.5, -2.0, -3.0, -4.0, -6.0])


def pack_weight(w, fmt):
    k, n = w.shape
    w = f64(bf(w)).reshape(k // 32, 32, n)
    amax = np.abs(w).max(1)
    if fmt == "e4m3":
        byte = np.frexp(amax)[1] - 1 + 127 - 7
    else:
        mant, ex = np.frexp(amax / 6.0)
        byte = np.where(mant > 0.5, ex, ex - 1) + 127
    byte = np.clip(np.where(amax > 0, byte, 1), 1, 254)
    scaled = (w * np.exp2(127.0 - byte)[:, None, :]).reshape(k, n).astype(np.float32)
    by_word = np.ascontiguousarray(scaled.reshape(k // 512, 128, 4, n).transpose(0, 1, 3, 2))
    if fmt == "e4m3":
        words = by_word.astype(ml_dtypes.float8_e4m3fn).view(np.uint8)
    else:
        c = by_word.astype(ml_dtypes.float4_e2m1fn).view(np.uint8) & 0xF
        words = c[..., 0::2] | (c[..., 1::2] << 4)
    return np.ascontiguousarray(words), np.ascontiguousarray(byte.astype(np.uint8).reshape(k // 512, 16, n))


def unpack_weight(words, scales, fmt):
    g, p, n, _ = words.shape
    if fmt == "e4m3":
        vals = np.ascontiguousarray(words).view(ml_dtypes.float8_e4m3fn).astype(np.float64)
    else:
        nib = np.empty((g, p, n, 4), np.uint8)
        nib[..., 0::2] = words & 0xF
        nib[..., 1::2] = words >> 4
        vals = E2M1[nib]
    vals = vals * np.repeat(np.exp2(scales.astype(np.float64) - 127.0), 8, axis=1)[..., None]
    return vals.transpose(0, 1, 3, 2).reshape(g * 512, n)
def pack4(w):
    words, scales = pack_weight(w, "e2m1")
    return words.reshape(words.shape[0], 128, -1), scales


def unpack4(words, scales):
    return unpack_weight(words.reshape(words.shape[0], 128, -1, 2), scales, "e2m1")


def planes(Y):
    n, m = Y.shape
    b = f64(bf(Y)).reshape(n // 32, 32, m)
    amax = np.abs(b).max(1)
    byte = np.clip(np.where(amax > 0, np.frexp(amax)[1] - 1 + 127 - 7, 1), 1, 254)
    codes = (b * np.exp2(127.0 - byte)[:, None, :]).reshape(n, m).astype(np.float32).astype(ml_dtypes.float8_e4m3fn).view(np.uint8)
    words = codes.reshape(n // 512, 128, 4, m).transpose(0, 1, 3, 2)
    return np.ascontiguousarray(words), np.ascontiguousarray(byte.astype(np.uint8).reshape(n // 512, 16, m))


M, R = 1024, 1024


def route_upstream(flow, nq, e):
    return mxq(flow * e, 1, "e4m3") @ nq


def setup_inputs():
    s = mx_kscale(R)
    q = np.random.standard_normal((M, R))
    qe = np.random.standard_normal((M, R))
    n = np.random.standard_normal((R, R)) / np.sqrt(R)
    e = 1.0 + 0.1 * np.random.standard_normal(R)
    c1 = np.random.uniform(0.2, 0.4, R)
    c2 = np.random.uniform(0.3, 0.5, R)
    n_words, n_scales = pack4(n / s[:, None])
    return {"q": bf(q), "qe": bf(qe), "n_words": n_words, "n_scales": n_scales, "e": bf(e * s), "c1": bf(c1), "c2": bf(c2)}


def core(q, qe, n_words, n_scales, e, c1, c2):
    q, qe, e, c1, c2 = f64(q), f64(qe), f64(e), f64(c1), f64(c2)
    nq = unpack4(n_words, n_scales)
    a = route_upstream(q, nq, e)
    c3 = 1.0 - c1 - c2
    b = c1 * qe + c2 * (a + qe) + c3 * q
    d = route_upstream(b, nq, e)
    return b + c1 * d


def reference(q, qe, n_words, n_scales, e, c1, c2):
    R_out = core(q, qe, n_words, n_scales, e, c1, c2)
    words, scales = planes(R_out)
    return R_out, words, scales

@@ -1,0 +1,460 @@
+from contextlib import ExitStack
+
+import concourse.mybir as mybir
+from concourse.masks import make_identity
+
+M, R = 1024, 1024
+FLOPS = 2 * 2 * M * R * R
+
+F32 = mybir.dt.float32
+BF16 = mybir.dt.bfloat16
+I32 = mybir.dt.int32
+U32 = mybir.dt.uint32
+U8 = mybir.dt.uint8
+FP8X4 = mybir.dt.float8_e4m3fn_x4
+FP4X4 = mybir.dt.float4_e2m1fn_x4
+MULT = mybir.AluOpType.mult
+ADD = mybir.AluOpType.add
+SUB = mybir.AluOpType.subtract
+COPY = mybir.ActivationFunctionType.Copy
+
+P = 128
+
+
+def tile_muskingumnetworktwotermneumannrouting_x2_kernel(
+    tc, q, qe, n_words, n_scales, e, c1, c2, out_0, out_1, out_2
+):
+    nc = tc.nc
+    with ExitStack() as ctx:
+        keep = ctx.enter_context(tc.tile_pool(name="keep", bufs=1))
+        work = ctx.enter_context(tc.tile_pool(name="work", bufs=2))
+        psum = ctx.enter_context(tc.psum_pool(name="psum", bufs=8))
+        ctx.enter_context(tc.manual_schedule())
+
+        def kt(name, shape, dtype):
+            return keep.tile(shape, dtype, name=name, tag=name, align_bytes=64)
+
+        def wt(name, shape, dtype, bufs):
+            return work.tile(shape, dtype, name=name, tag=name, bufs=bufs, align_bytes=64)
+
+        ident = kt("ident", [P, P], F32)
+        vec_e = kt("vec_e", [P, 2, 4], BF16)
+        vec_1 = kt("vec_1", [P, 2, 4], BF16)
+        vec_2 = kt("vec_2", [P, 2, 4], BF16)
+        col_e = kt("col_e", [P, 2, 4], F32)
+        col_1 = kt("col_1", [P, 2, 4], F32)
+        col_2 = kt("col_2", [P, 2, 4], F32)
+        col_12 = kt("col_12", [P, 2, 4], F32)
+        col_3 = kt("col_3", [P, 2, 4], F32)
+        n_raw = kt("n_raw", [P, 2, 2048], U8)
+        n_per = kt("n_per", [P, 2, 2048], U8)
+        s_raw = kt("s_raw", [P, 2, 1024], U8)
+        s_per = kt("s_per", [P, 2, 1024], U8)
+        q_sb = [kt("q_sb%d" % G, [P, 4, R], BF16) for G in range(2)]
+        qe_sb = [kt("qe_sb%d" % G, [P, 4, R], BF16) for G in range(2)]
+        bb = {}
+        xc = {}
+        xs = {}
+        bc = {}
+        bs = {}
+        for G in range(2):
+            for g in range(2):
+                bb[G, g] = kt("bb%d%d" % (G, g), [P, 4, 512], F32)
+                xc[G, g] = kt("xc%d%d" % (G, g), [P, 512], U32)
+                xs[G, g] = kt("xs%d%d" % (G, g), [P, 512], U8)
+                bc[G, g] = kt("bc%d%d" % (G, g), [P, 512], U32)
+                bs[G, g] = kt("bs%d%d" % (G, g), [P, 512], U8)
+
+        nc.gpsimd.memset(s_raw[:].rearrange("p g c -> p (g c)").bitcast(I32), 0)
+
+        def load_rows(dst, src, G, tp):
+            rows = src[512 * G : 512 * G + 512, :].rearrange("(p t) k -> p t k", t=4)
+            nc.sync.dma_start(out=dst[G][:, 2 * tp : 2 * tp + 2, :], in_=rows[:, 2 * tp : 2 * tp + 2, :])
+
+        for src, dst in ((e, vec_e), (c1, vec_1), (c2, vec_2)):
+            nc.scalar.dma_start(out=dst[:], in_=src.rearrange("(g p t) -> p g t", g=2, t=4))
+        for Q in range(4):
+            nc.scalar.dma_start(
+                out=s_raw[32 * Q : 32 * Q + 4, :, :].bitcast(I32),
+                in_=n_scales[:, 4 * Q : 4 * Q + 4, :].rearrange("g q c -> q g c").bitcast(I32),
+            )
+        for g in range(2):
+            nc.sync.dma_start(out=n_raw[:, g, :].bitcast(I32), in_=n_words[g].bitcast(I32))
+        load_rows(q_sb, q, 0, 0)
+        load_rows(q_sb, q, 0, 1)
+        load_rows(qe_sb, qe, 0, 0)
+        load_rows(qe_sb, qe, 0, 1)
+        load_rows(q_sb, q, 1, 0)
+        load_rows(q_sb, q, 1, 1)
+        load_rows(qe_sb, qe, 1, 0)
+        load_rows(qe_sb, qe, 1, 1)
+
+        make_identity(nc, ident[:])
+        nc.gpsimd.tensor_tensor(out=col_12[:], in0=vec_1[:], in1=vec_2[:], op=ADD)
+        nc.gpsimd.tensor_scalar(out=col_3[:], in0=col_12[:], scalar1=-1.0, scalar2=1.0, op0=MULT, op1=ADD)
+        for col, vec in ((col_e, vec_e), (col_1, vec_1), (col_2, vec_2)):
+            nc.scalar.activation(out=col[:], in_=vec[:], func=COPY)
+
+        def permute_words(g, h):
+            nc.vector.tensor_copy(
+                out=n_per[:, g, 1024 * h : 1024 * h + 1024].rearrange("p (t m b) -> p t m b", t=4, b=2),
+                in_=n_raw[:, g, 1024 * h : 1024 * h + 1024].rearrange("p (m t b) -> p t m b", t=4, b=2),
+            )
+
+        def permute_scales(h):
+            nc.vector.tensor_copy(
+                out=s_per[:, :, 512 * h : 512 * h + 512].rearrange("p g (t m) -> p g t m", t=4),
+                in_=s_raw[:, :, 512 * h : 512 * h + 512].rearrange("p g (m t) -> p g t m", t=4),
+            )
+
+        def turn_q(G, tp, g):
+            bank = psum.tile([P, 2, 256], F32, name="bank", tag="bank", bufs=8)
+            for u in range(2):
+                for s in range(2):
+                    words = q_sb[G][:, 2 * tp + s, :].bitcast(F32)
+                    nc.tensor.transpose(
+                        bank[:, u, 128 * s : 128 * s + 128], words[:, 256 * g + u : 256 * g + 256 : 2], ident[:]
+                    )
+            return bank
+
+        def turn_qe(G, g, u):
+            bank = psum.tile([P, 512], F32, name="bank", tag="bank", bufs=8)
+            for s in range(4):
+                words = qe_sb[G][:, s, :].bitcast(F32)
+                nc.tensor.transpose(
+                    bank[:, 128 * s : 128 * s + 128], words[:, 256 * g + u : 256 * g + 256 : 2], ident[:]
+                )
+            return bank
+
+        xb = {}
+
+        def make_x(bank, G, tp, g):
+            if tp == 0:
+                xb[G, g] = wt("xb", [P, 512, 4], BF16, 4)
+            nc.vector.tensor_tensor(
+                out=xb[G, g][:, 256 * tp : 256 * tp + 256, :].rearrange("p j (u w) -> p j u w", u=2),
+                in0=bank[:].bitcast(BF16).rearrange("p u (j w) -> p j u w", w=2),
+                in1=vec_e[:, g, :].rearrange("p (u w) -> p u w", u=2).unsqueeze(1).to_broadcast([P, 256, 2, 2]),
+                op=MULT,
+            )
+
+        def make_c3q(bank, G, tp, g):
+            view = bank[:].bitcast(BF16).rearrange("p u (j w) -> p u j w", w=2)
+            for u in range(2):
+                for w in range(2):
+                    t = 2 * u + w
+                    nc.scalar.activation(
+                        out=bb[G, g][:, t, 256 * tp : 256 * tp + 256],
+                        in_=view[:, u, :, w],
+                        func=COPY,
+                        scale=col_3[:, g, t : t + 1],
+                    )
+
+        def quant(codes, scales, tile4):
+            nc.vector.quantize_mx(
+                out=codes[:].bitcast(FP8X4), scales=scales[:], in_=tile4[:].rearrange("p j t -> p (j t)")
+            )
+
+        def add_qe(bank, G, g, u):
+            view = bank[:].bitcast(BF16).rearrange("p (j w) -> p j w", w=2)
+            for w in range(2):
+                t = 2 * u + w
+                nc.vector.scalar_tensor_tensor(
+                    out=bb[G, g][:, t, :],
+                    in0=view[:, :, w],
+                    scalar=col_12[:, g, t : t + 1],
+                    in1=bb[G, g][:, t, :],
+                    op0=MULT,
+                    op1=ADD,
+                )
+
+        def half_product(bank, codes, scales, G, g, t, k):
+            nc.tensor.matmul_mx(
+                out=bank[:],
+                lhsT=n_per[:, k, 1024 * g + 256 * t : 1024 * g + 256 * t + 256].bitcast(FP4X4),
+                lhsT_scale=s_per[:, k, 512 * g + 128 * t : 512 * g + 128 * t + 128],
+                rhs=codes[G, k][:].bitcast(FP8X4),
+                rhs_scale=scales[G, k][:],
+                start=(k == 0),
+                stop=(k == 1),
+            )
+
+        def product(tag, codes, scales, G, g, t):
+            bank = psum.tile([P, 512], F32, name="bank", tag="bank", bufs=8)
+            for k in range(2):
+                half_product(bank, codes, scales, G, g, t, k)
+            return bank
+
+        def accum(bank, col, G, g, t):
+            nc.vector.scalar_tensor_tensor(
+                out=bb[G, g][:, t, :],
+                in0=bank[:],
+                scalar=col[:, g, t : t + 1],
+                in1=bb[G, g][:, t, :],
+                op0=MULT,
+                op1=ADD,
+            )
+
+        eb = {}
+
+        def pre_be(G, g, t):
+            if t == 0:
+                eb[G, g] = wt("eb", [P, 4, 512], F32, 2)
+            nc.scalar.activation(
+                out=eb[G, g][:, t, :], in_=bb[G, g][:, t, :], func=COPY, scale=col_e[:, g, t : t + 1]
+            )
+
+        def lay_be(G, g):
+            tile4 = wt("be", [P, 512, 4], BF16, 4)
+            nc.vector.tensor_copy(out=tile4[:], in_=eb[G, g][:].rearrange("p t j -> p j t"))
+            return tile4
+
+        cd = {}
+        of = {}
+        ob = {}
+        be = {}
+        to = {}
+        tq = {}
+        tqe = {}
+        mm = {}
+        dd = {}
+
+        def scale_d(bank, G, g, t):
+            if (G, g) not in cd:
+                cd[G, g] = wt("cd", [P, 4, 512], F32, 2)
+            nc.scalar.activation(out=cd[G, g][:, t, :], in_=bank[:], func=COPY, scale=col_1[:, g, t : t + 1])
+
+        def turn_out(G, g, s, by_pe):
+            bank = psum.tile([P, 4, P], F32, name="bank", tag="bank", bufs=8)
+            cols = slice(128 * s, 128 * s + 128)
+            for t in range(4):
+                nc.tensor.matmul(
+                    out=bank[:, t, :], lhsT=bb[G, g][:, t, cols], rhs=ident[:],
+                    start=True, stop=not by_pe[t], is_transpose=True,
+                )
+                if by_pe[t]:
+                    nc.tensor.matmul(
+                        out=bank[:, t, :], lhsT=cd[G, g][:, t, cols], rhs=ident[:],
+                        start=False, stop=True, is_transpose=True,
+                    )
+            return bank
+
+        def evac(bank, G, g, s, on_scalar):
+            if (G, g) not in of:
+                of[G, g] = wt("of", [P, 4, 512], F32, 4)
+            dst = of[G, g][:, s, :].rearrange("p (c t) -> p c t", t=4)
+            src = bank[:].rearrange("p t c -> p c t")
+            if on_scalar:
+                nc.scalar.copy(out=dst, in_=src)
+            else:
+                nc.vector.tensor_copy(out=dst, in_=src)
+            if (G, s) == (0, 3):
+                store_rows(G, g, 0, 4)
+            if G == 1 and s % 2 == 1:
+                store_rows(G, g, s - 1, s + 1)
+
+        def store_rows(G, g, s0, s1):
+            rows = out_0[512 * G : 512 * G + 512, 512 * g : 512 * g + 512].rearrange("(p t) r -> p t r", t=4)
+            nc.sync.dma_start(out=rows[:, s0:s1, :], in_=of[G, g][:, s0:s1, :])
+
+        def cast_out(G, g, on_scalar):
+            tile4 = wt("ob", [P, 512, 4], BF16, 2)
+            src = of[G, g][:].rearrange("p t r -> p r t")
+            if on_scalar:
+                nc.scalar.copy(out=tile4[:], in_=src)
+            else:
+                nc.vector.tensor_copy(out=tile4[:], in_=src)
+            return tile4
+
+        def store_planes(ob, G, g):
+            oc = wt("oc", [P, 512], U32, 4)
+            osc = wt("osc", [P, 512], U8, 4)
+            quant(oc, osc, ob)
+            nc.sync.dma_start(
+                out=out_1[G, :, 512 * g : 512 * g + 512, :].rearrange("p m t -> p (m t)").bitcast(I32),
+                in_=oc[:].bitcast(I32),
+            )
+            for Q in range(4):
+                nc.sync.dma_start(
+                    out=out_2[G, 4 * Q : 4 * Q + 4, 512 * g : 512 * g + 512].bitcast(I32),
+                    in_=osc[32 * Q : 32 * Q + 4, :].bitcast(I32),
+                )
+
+        tq[0, 0, 0] = turn_q(0, 0, 0)
+        permute_words(0, 0)
+        permute_words(0, 1)
+        permute_words(1, 0)
+        permute_words(1, 1)
+        tq[0, 0, 1] = turn_q(0, 0, 1)
+        tq[0, 1, 0] = turn_q(0, 1, 0)
+        tq[0, 1, 1] = turn_q(0, 1, 1)
+        make_x(tq[0, 0, 0], 0, 0, 0)
+        make_c3q(tq[0, 0, 0], 0, 0, 0)
+        make_x(tq[0, 0, 1], 0, 0, 1)
+        make_x(tq[0, 1, 0], 0, 1, 0)
+        make_c3q(tq[0, 1, 0], 0, 1, 0)
+        make_x(tq[0, 1, 1], 0, 1, 1)
+        make_c3q(tq[0, 0, 1], 0, 0, 1)
+        make_c3q(tq[0, 1, 1], 0, 1, 1)
+        quant(xc[0, 0], xs[0, 0], xb[0, 0])
+        quant(xc[0, 1], xs[0, 1], xb[0, 1])
+        tqe[0, 0, 0] = turn_qe(0, 0, 0)
+        tqe[0, 0, 1] = turn_qe(0, 0, 1)
+        tq[1, 0, 0] = turn_q(1, 0, 0)
+        tq[1, 0, 1] = turn_q(1, 0, 1)
+        tqe[0, 1, 0] = turn_qe(0, 1, 0)
+        tqe[0, 1, 1] = turn_qe(0, 1, 1)
+        permute_scales(0)
+        permute_scales(1)
+        make_x(tq[1, 0, 0], 1, 0, 0)
+        make_c3q(tq[1, 0, 0], 1, 0, 0)
+        add_qe(tqe[0, 0, 0], 0, 0, 0)
+        make_x(tq[1, 0, 1], 1, 0, 1)
+        make_c3q(tq[1, 0, 1], 1, 0, 1)
+        add_qe(tqe[0, 0, 1], 0, 0, 1)
+        mm[0, 0, 0] = product("mm", xc, xs, 0, 0, 0)
+        mm[0, 0, 1] = product("mm", xc, xs, 0, 0, 1)
+        mm[0, 0, 2] = product("mm", xc, xs, 0, 0, 2)
+        mm[0, 0, 3] = product("mm", xc, xs, 0, 0, 3)
+        accum(mm[0, 0, 0], col_2, 0, 0, 0)
+        pre_be(0, 0, 0)
+        accum(mm[0, 0, 1], col_2, 0, 0, 1)
+        pre_be(0, 0, 1)
+        accum(mm[0, 0, 2], col_2, 0, 0, 2)
+        pre_be(0, 0, 2)
+        accum(mm[0, 0, 3], col_2, 0, 0, 3)
+        pre_be(0, 0, 3)
+        mm[0, 1, 0] = product("mm", xc, xs, 0, 1, 0)
+        mm[0, 1, 1] = product("mm", xc, xs, 0, 1, 1)
+        mm[0, 1, 2] = product("mm", xc, xs, 0, 1, 2)
+        mm[0, 1, 3] = product("mm", xc, xs, 0, 1, 3)
+        add_qe(tqe[0, 1, 0], 0, 1, 0)
+        add_qe(tqe[0, 1, 1], 0, 1, 1)
+        tq[1, 1, 0] = turn_q(1, 1, 0)
+        tq[1, 1, 1] = turn_q(1, 1, 1)
+        accum(mm[0, 1, 0], col_2, 0, 1, 0)
+        pre_be(0, 1, 0)
+        accum(mm[0, 1, 1], col_2, 0, 1, 1)
+        pre_be(0, 1, 1)
+        accum(mm[0, 1, 2], col_2, 0, 1, 2)
+        pre_be(0, 1, 2)
+        accum(mm[0, 1, 3], col_2, 0, 1, 3)
+        pre_be(0, 1, 3)
+        make_x(tq[1, 1, 0], 1, 1, 0)
+        make_c3q(tq[1, 1, 0], 1, 1, 0)
+        be[0, 0] = lay_be(0, 0)
+        be[0, 1] = lay_be(0, 1)
+        quant(bc[0, 0], bs[0, 0], be[0, 0])
+        make_x(tq[1, 1, 1], 1, 1, 1)
+        make_c3q(tq[1, 1, 1], 1, 1, 1)
+        quant(bc[0, 1], bs[0, 1], be[0, 1])
+        quant(xc[1, 0], xs[1, 0], xb[1, 0])
+        quant(xc[1, 1], xs[1, 1], xb[1, 1])
+        tqe[1, 0, 0] = turn_qe(1, 0, 0)
+        tqe[1, 0, 1] = turn_qe(1, 0, 1)
+        dd[0, 0, 0] = product("dd", bc, bs, 0, 0, 0)
+        dd[0, 0, 1] = product("dd", bc, bs, 0, 0, 1)
+        dd[0, 0, 2] = product("dd", bc, bs, 0, 0, 2)
+        dd[0, 0, 3] = product("dd", bc, bs, 0, 0, 3)
+        add_qe(tqe[1, 0, 0], 1, 0, 0)
+        add_qe(tqe[1, 0, 1], 1, 0, 1)
+        mm[1, 0, 0] = product("mm", xc, xs, 1, 0, 0)
+        mm[1, 0, 1] = product("mm", xc, xs, 1, 0, 1)
+        mm[1, 0, 2] = product("mm", xc, xs, 1, 0, 2)
+        mm[1, 0, 3] = product("mm", xc, xs, 1, 0, 3)
+        scale_d(dd[0, 0, 0], 0, 0, 0)
+        scale_d(dd[0, 0, 1], 0, 0, 1)
+        scale_d(dd[0, 0, 2], 0, 0, 2)
+        scale_d(dd[0, 0, 3], 0, 0, 3)
+        accum(mm[1, 0, 0], col_2, 1, 0, 0)
+        pre_be(1, 0, 0)
+        accum(mm[1, 0, 1], col_2, 1, 0, 1)
+        pre_be(1, 0, 1)
+        accum(mm[1, 0, 2], col_2, 1, 0, 2)
+        pre_be(1, 0, 2)
+        accum(mm[1, 0, 3], col_2, 1, 0, 3)
+        pre_be(1, 0, 3)
+        tqe[1, 1, 0] = turn_qe(1, 1, 0)
+        tqe[1, 1, 1] = turn_qe(1, 1, 1)
+        dd[0, 1, 0] = product("dd", bc, bs, 0, 1, 0)
+        dd[0, 1, 1] = product("dd", bc, bs, 0, 1, 1)
+        dd[0, 1, 2] = product("dd", bc, bs, 0, 1, 2)
+        dd[0, 1, 3] = product("dd", bc, bs, 0, 1, 3)
+        add_qe(tqe[1, 1, 0], 1, 1, 0)
+        add_qe(tqe[1, 1, 1], 1, 1, 1)
+        mm[1, 1, 0] = product("mm", xc, xs, 1, 1, 0)
+        mm[1, 1, 1] = product("mm", xc, xs, 1, 1, 1)
+        mm[1, 1, 2] = product("mm", xc, xs, 1, 1, 2)
+        mm[1, 1, 3] = product("mm", xc, xs, 1, 1, 3)
+        scale_d(dd[0, 1, 0], 0, 1, 0)
+        scale_d(dd[0, 1, 1], 0, 1, 1)
+        scale_d(dd[0, 1, 2], 0, 1, 2)
+        scale_d(dd[0, 1, 3], 0, 1, 3)
+        accum(mm[1, 1, 0], col_2, 1, 1, 0)
+        pre_be(1, 1, 0)
+        accum(mm[1, 1, 1], col_2, 1, 1, 1)
+        pre_be(1, 1, 1)
+        accum(mm[1, 1, 2], col_2, 1, 1, 2)
+        pre_be(1, 1, 2)
+        accum(mm[1, 1, 3], col_2, 1, 1, 3)
+        pre_be(1, 1, 3)
+        to[0, 0, 0] = turn_out(0, 0, 0, [True, True, True, True])
+        to[0, 0, 1] = turn_out(0, 0, 1, [True, True, True, True])
+        to[0, 0, 2] = turn_out(0, 0, 2, [True, True, True, True])
+        to[0, 0, 3] = turn_out(0, 0, 3, [True, True, True, True])
+        evac(to[0, 0, 0], 0, 0, 0, True)
+        evac(to[0, 0, 1], 0, 0, 1, True)
+        evac(to[0, 0, 2], 0, 0, 2, True)
+        evac(to[0, 0, 3], 0, 0, 3, True)
+        be[1, 0] = lay_be(1, 0)
+        be[1, 1] = lay_be(1, 1)
+        quant(bc[1, 0], bs[1, 0], be[1, 0])
+        to[0, 1, 0] = turn_out(0, 1, 0, [True, True, True, True])
+        to[0, 1, 1] = turn_out(0, 1, 1, [True, True, True, True])
+        quant(bc[1, 1], bs[1, 1], be[1, 1])
+        dd[1, 0, 0] = product("dd", bc, bs, 1, 0, 0)
+        dd[1, 0, 1] = product("dd", bc, bs, 1, 0, 1)
+        dd[1, 0, 2] = product("dd", bc, bs, 1, 0, 2)
+        dd[1, 0, 3] = product("dd", bc, bs, 1, 0, 3)
+        to[0, 1, 2] = turn_out(0, 1, 2, [True, True, True, True])
+        to[0, 1, 3] = turn_out(0, 1, 3, [True, True, True, True])
+        evac(to[0, 1, 0], 0, 1, 0, True)
+        evac(to[0, 1, 1], 0, 1, 1, True)
+        evac(to[0, 1, 2], 0, 1, 2, True)
+        evac(to[0, 1, 3], 0, 1, 3, True)
+        ob[0, 0] = cast_out(0, 0, False)
+        accum(dd[1, 0, 0], col_1, 1, 0, 0)
+        accum(dd[1, 0, 1], col_1, 1, 0, 1)
+        accum(dd[1, 0, 2], col_1, 1, 0, 2)
+        accum(dd[1, 0, 3], col_1, 1, 0, 3)
+        dd[1, 1, 0] = product("dd", bc, bs, 1, 1, 0)
+        dd[1, 1, 1] = product("dd", bc, bs, 1, 1, 1)
+        dd[1, 1, 2] = product("dd", bc, bs, 1, 1, 2)
+        dd[1, 1, 3] = product("dd", bc, bs, 1, 1, 3)
+        store_planes(ob[0, 0], 0, 0)
+        to[1, 0, 0] = turn_out(1, 0, 0, [False, False, False, False])
+        to[1, 0, 1] = turn_out(1, 0, 1, [False, False, False, False])
+        to[1, 0, 2] = turn_out(1, 0, 2, [False, False, False, False])
+        to[1, 0, 3] = turn_out(1, 0, 3, [False, False, False, False])
+        scale_d(dd[1, 1, 0], 1, 1, 0)
+        scale_d(dd[1, 1, 1], 1, 1, 1)
+        scale_d(dd[1, 1, 2], 1, 1, 2)
+        scale_d(dd[1, 1, 3], 1, 1, 3)
+        ob[0, 1] = cast_out(0, 1, False)
+        evac(to[1, 0, 0], 1, 0, 0, True)
+        evac(to[1, 0, 1], 1, 0, 1, True)
+        evac(to[1, 0, 2], 1, 0, 2, True)
+        evac(to[1, 0, 3], 1, 0, 3, True)
+        store_planes(ob[0, 1], 0, 1)
+        to[1, 1, 0] = turn_out(1, 1, 0, [True, True, True, True])
+        to[1, 1, 1] = turn_out(1, 1, 1, [True, True, True, True])
+        to[1, 1, 2] = turn_out(1, 1, 2, [True, True, True, True])
+        to[1, 1, 3] = turn_out(1, 1, 3, [True, True, True, True])
+        evac(to[1, 1, 0], 1, 1, 0, False)
+        evac(to[1, 1, 1], 1, 1, 1, True)
+        evac(to[1, 1, 2], 1, 1, 2, False)
+        evac(to[1, 1, 3], 1, 1, 3, True)
+        ob[1, 0] = cast_out(1, 0, False)
+        store_planes(ob[1, 0], 1, 0)
+        ob[1, 1] = cast_out(1, 1, False)
+        store_planes(ob[1, 1], 1, 1)

@@ -129,7 +129,7 @@ def tile_muskingumnetworktwotermneumannrouting_x2_kernel(
         xb = {}
 
         def make_x(bank, G, tp, g):
-            if tp == 0:
+            if (G, g) not in xb:
                 xb[G, g] = wt("xb", [P, 512, 4], BF16, 4)
             nc.vector.tensor_tensor(
                 out=xb[G, g][:, 256 * tp : 256 * tp + 256, :].rearrange("p j (u w) -> p j u w", u=2),
@@ -195,18 +195,28 @@ def tile_muskingumnetworktwotermneumannrouting_x2_kernel(
                 op1=ADD,
             )
 
+        def by_four(tile4):
+            return tile4[:].rearrange("p (c i) t -> p c t i", i=4)
+
         eb = {}
 
-        def pre_be(G, g, t):
+        def pre_be(G, g, t, on_scalar):
             if t == 0:
                 eb[G, g] = wt("eb", [P, 4, 512], F32, 2)
-            nc.scalar.activation(
-                out=eb[G, g][:, t, :], in_=bb[G, g][:, t, :], func=COPY, scale=col_e[:, g, t : t + 1]
-            )
+            if on_scalar:
+                nc.scalar.activation(
+                    out=eb[G, g][:, t, :], in_=bb[G, g][:, t, :], func=COPY, scale=col_e[:, g, t : t + 1]
+                )
+            else:
+                nc.gpsimd.tensor_scalar(
+                    out=eb[G, g][:, t, :], in0=bb[G, g][:, t, :], scalar1=col_e[:, g, t : t + 1],
+                    scalar2=0.0, op0=MULT, op1=ADD,
+                )
 
-        def lay_be(G, g):
+        def lay_be(G, g, on_scalar):
             tile4 = wt("be", [P, 512, 4], BF16, 4)
-            nc.vector.tensor_copy(out=tile4[:], in_=eb[G, g][:].rearrange("p t j -> p j t"))
+            copy = nc.scalar.copy if on_scalar else nc.vector.tensor_copy
+            copy(out=by_four(tile4), in_=eb[G, g][:].rearrange("p t (c i) -> p c t i", i=4))
             return tile4
 
         cd = {}
@@ -259,11 +269,11 @@ def tile_muskingumnetworktwotermneumannrouting_x2_kernel(
 
         def cast_out(G, g, on_scalar):
             tile4 = wt("ob", [P, 512, 4], BF16, 2)
-            src = of[G, g][:].rearrange("p t r -> p r t")
+            src = of[G, g][:].rearrange("p t (c i) -> p c t i", i=4)
             if on_scalar:
-                nc.scalar.copy(out=tile4[:], in_=src)
+                nc.scalar.copy(out=by_four(tile4), in_=src)
             else:
-                nc.vector.tensor_copy(out=tile4[:], in_=src)
+                nc.vector.tensor_copy(out=by_four(tile4), in_=src)
             return tile4
 
         def store_planes(ob, G, g):
@@ -280,181 +290,181 @@ def tile_muskingumnetworktwotermneumannrouting_x2_kernel(
                     in_=osc[32 * Q : 32 * Q + 4, :].bitcast(I32),
                 )
 
-        tq[0, 0, 0] = turn_q(0, 0, 0)
         permute_words(0, 0)
-        permute_words(0, 1)
         permute_words(1, 0)
-        permute_words(1, 1)
+        tq[0, 0, 0] = turn_q(0, 0, 0)
         tq[0, 0, 1] = turn_q(0, 0, 1)
+        permute_words(0, 1)
+        permute_words(1, 1)
+        make_x(tq[0, 0, 0], 0, 0, 0)
+        make_x(tq[0, 0, 1], 0, 0, 1)
+        make_c3q(tq[0, 0, 0], 0, 0, 0)
+        make_c3q(tq[0, 0, 1], 0, 0, 1)
         tq[0, 1, 0] = turn_q(0, 1, 0)
         tq[0, 1, 1] = turn_q(0, 1, 1)
-        make_x(tq[0, 0, 0], 0, 0, 0)
-        make_c3q(tq[0, 0, 0], 0, 0, 0)
-        make_x(tq[0, 0, 1], 0, 0, 1)
-        make_x(tq[0, 1, 0], 0, 1, 0)
-        make_c3q(tq[0, 1, 0], 0, 1, 0)
-        make_x(tq[0, 1, 1], 0, 1, 1)
-        make_c3q(tq[0, 0, 1], 0, 0, 1)
-        make_c3q(tq[0, 1, 1], 0, 1, 1)
-        quant(xc[0, 0], xs[0, 0], xb[0, 0])
-        quant(xc[0, 1], xs[0, 1], xb[0, 1])
         tqe[0, 0, 0] = turn_qe(0, 0, 0)
         tqe[0, 0, 1] = turn_qe(0, 0, 1)
-        tq[1, 0, 0] = turn_q(1, 0, 0)
-        tq[1, 0, 1] = turn_q(1, 0, 1)
+        make_x(tq[0, 1, 0], 0, 1, 0)
+        make_x(tq[0, 1, 1], 0, 1, 1)
         tqe[0, 1, 0] = turn_qe(0, 1, 0)
         tqe[0, 1, 1] = turn_qe(0, 1, 1)
         permute_scales(0)
+        make_c3q(tq[0, 1, 0], 0, 1, 0)
+        make_c3q(tq[0, 1, 1], 0, 1, 1)
+        quant(xc[0, 0], xs[0, 0], xb[0, 0])
+        quant(xc[0, 1], xs[0, 1], xb[0, 1])
         permute_scales(1)
-        make_x(tq[1, 0, 0], 1, 0, 0)
-        make_c3q(tq[1, 0, 0], 1, 0, 0)
+        tq[1, 0, 0] = turn_q(1, 0, 0)
+        tq[1, 0, 1] = turn_q(1, 0, 1)
         add_qe(tqe[0, 0, 0], 0, 0, 0)
-        make_x(tq[1, 0, 1], 1, 0, 1)
-        make_c3q(tq[1, 0, 1], 1, 0, 1)
         add_qe(tqe[0, 0, 1], 0, 0, 1)
+        tq[1, 1, 0] = turn_q(1, 1, 0)
+        tq[1, 1, 1] = turn_q(1, 1, 1)
+        add_qe(tqe[0, 1, 0], 0, 1, 0)
+        add_qe(tqe[0, 1, 1], 0, 1, 1)
+        make_c3q(tq[1, 1, 0], 1, 1, 0)
+        make_c3q(tq[1, 1, 1], 1, 1, 1)
+        mm[0, 1, 0] = product("mm", xc, xs, 0, 1, 0)
+        mm[0, 1, 1] = product("mm", xc, xs, 0, 1, 1)
+        mm[0, 1, 2] = product("mm", xc, xs, 0, 1, 2)
+        mm[0, 1, 3] = product("mm", xc, xs, 0, 1, 3)
+        accum(mm[0, 1, 0], col_2, 0, 1, 0)
+        accum(mm[0, 1, 1], col_2, 0, 1, 1)
+        accum(mm[0, 1, 2], col_2, 0, 1, 2)
+        accum(mm[0, 1, 3], col_2, 0, 1, 3)
+        make_c3q(tq[1, 0, 0], 1, 0, 0)
+        make_c3q(tq[1, 0, 1], 1, 0, 1)
         mm[0, 0, 0] = product("mm", xc, xs, 0, 0, 0)
         mm[0, 0, 1] = product("mm", xc, xs, 0, 0, 1)
         mm[0, 0, 2] = product("mm", xc, xs, 0, 0, 2)
         mm[0, 0, 3] = product("mm", xc, xs, 0, 0, 3)
         accum(mm[0, 0, 0], col_2, 0, 0, 0)
-        pre_be(0, 0, 0)
         accum(mm[0, 0, 1], col_2, 0, 0, 1)
-        pre_be(0, 0, 1)
         accum(mm[0, 0, 2], col_2, 0, 0, 2)
-        pre_be(0, 0, 2)
         accum(mm[0, 0, 3], col_2, 0, 0, 3)
-        pre_be(0, 0, 3)
-        mm[0, 1, 0] = product("mm", xc, xs, 0, 1, 0)
-        mm[0, 1, 1] = product("mm", xc, xs, 0, 1, 1)
-        mm[0, 1, 2] = product("mm", xc, xs, 0, 1, 2)
-        mm[0, 1, 3] = product("mm", xc, xs, 0, 1, 3)
-        add_qe(tqe[0, 1, 0], 0, 1, 0)
-        add_qe(tqe[0, 1, 1], 0, 1, 1)
-        tq[1, 1, 0] = turn_q(1, 1, 0)
-        tq[1, 1, 1] = turn_q(1, 1, 1)
-        accum(mm[0, 1, 0], col_2, 0, 1, 0)
-        pre_be(0, 1, 0)
-        accum(mm[0, 1, 1], col_2, 0, 1, 1)
-        pre_be(0, 1, 1)
-        accum(mm[0, 1, 2], col_2, 0, 1, 2)
-        pre_be(0, 1, 2)
-        accum(mm[0, 1, 3], col_2, 0, 1, 3)
-        pre_be(0, 1, 3)
-        make_x(tq[1, 1, 0], 1, 1, 0)
-        make_c3q(tq[1, 1, 0], 1, 1, 0)
-        be[0, 0] = lay_be(0, 0)
-        be[0, 1] = lay_be(0, 1)
-        quant(bc[0, 0], bs[0, 0], be[0, 0])
-        make_x(tq[1, 1, 1], 1, 1, 1)
-        make_c3q(tq[1, 1, 1], 1, 1, 1)
-        quant(bc[0, 1], bs[0, 1], be[0, 1])
-        quant(xc[1, 0], xs[1, 0], xb[1, 0])
-        quant(xc[1, 1], xs[1, 1], xb[1, 1])
-        tqe[1, 0, 0] = turn_qe(1, 0, 0)
-        tqe[1, 0, 1] = turn_qe(1, 0, 1)
-        dd[0, 0, 0] = product("dd", bc, bs, 0, 0, 0)
-        dd[0, 0, 1] = product("dd", bc, bs, 0, 0, 1)
-        dd[0, 0, 2] = product("dd", bc, bs, 0, 0, 2)
-        dd[0, 0, 3] = product("dd", bc, bs, 0, 0, 3)
-        add_qe(tqe[1, 0, 0], 1, 0, 0)
-        add_qe(tqe[1, 0, 1], 1, 0, 1)
-        mm[1, 0, 0] = product("mm", xc, xs, 1, 0, 0)
-        mm[1, 0, 1] = product("mm", xc, xs, 1, 0, 1)
-        mm[1, 0, 2] = product("mm", xc, xs, 1, 0, 2)
-        mm[1, 0, 3] = product("mm", xc, xs, 1, 0, 3)
-        scale_d(dd[0, 0, 0], 0, 0, 0)
-        scale_d(dd[0, 0, 1], 0, 0, 1)
-        scale_d(dd[0, 0, 2], 0, 0, 2)
-        scale_d(dd[0, 0, 3], 0, 0, 3)
-        accum(mm[1, 0, 0], col_2, 1, 0, 0)
-        pre_be(1, 0, 0)
-        accum(mm[1, 0, 1], col_2, 1, 0, 1)
-        pre_be(1, 0, 1)
-        accum(mm[1, 0, 2], col_2, 1, 0, 2)
-        pre_be(1, 0, 2)
-        accum(mm[1, 0, 3], col_2, 1, 0, 3)
-        pre_be(1, 0, 3)
         tqe[1, 1, 0] = turn_qe(1, 1, 0)
         tqe[1, 1, 1] = turn_qe(1, 1, 1)
-        dd[0, 1, 0] = product("dd", bc, bs, 0, 1, 0)
-        dd[0, 1, 1] = product("dd", bc, bs, 0, 1, 1)
-        dd[0, 1, 2] = product("dd", bc, bs, 0, 1, 2)
-        dd[0, 1, 3] = product("dd", bc, bs, 0, 1, 3)
+        pre_be(0, 1, 0, False)
+        pre_be(0, 1, 1, False)
+        pre_be(0, 1, 2, False)
+        pre_be(0, 1, 3, False)
+        be[0, 1] = lay_be(0, 1, True)
+        make_x(tq[1, 1, 0], 1, 1, 0)
+        make_x(tq[1, 1, 1], 1, 1, 1)
+        make_x(tq[1, 0, 0], 1, 0, 0)
+        make_x(tq[1, 0, 1], 1, 0, 1)
+        quant(bc[0, 1], bs[0, 1], be[0, 1])
+        tqe[1, 0, 0] = turn_qe(1, 0, 0)
+        tqe[1, 0, 1] = turn_qe(1, 0, 1)
+        quant(xc[1, 1], xs[1, 1], xb[1, 1])
+        pre_be(0, 0, 0, False)
+        pre_be(0, 0, 1, False)
+        pre_be(0, 0, 2, False)
+        pre_be(0, 0, 3, False)
+        quant(xc[1, 0], xs[1, 0], xb[1, 0])
+        be[0, 0] = lay_be(0, 0, True)
+        quant(bc[0, 0], bs[0, 0], be[0, 0])
         add_qe(tqe[1, 1, 0], 1, 1, 0)
         add_qe(tqe[1, 1, 1], 1, 1, 1)
         mm[1, 1, 0] = product("mm", xc, xs, 1, 1, 0)
         mm[1, 1, 1] = product("mm", xc, xs, 1, 1, 1)
         mm[1, 1, 2] = product("mm", xc, xs, 1, 1, 2)
         mm[1, 1, 3] = product("mm", xc, xs, 1, 1, 3)
+        accum(mm[1, 1, 0], col_2, 1, 1, 0)
+        accum(mm[1, 1, 1], col_2, 1, 1, 1)
+        accum(mm[1, 1, 2], col_2, 1, 1, 2)
+        accum(mm[1, 1, 3], col_2, 1, 1, 3)
+        dd[0, 1, 0] = product("dd", bc, bs, 0, 1, 0)
+        dd[0, 1, 1] = product("dd", bc, bs, 0, 1, 1)
+        dd[0, 1, 2] = product("dd", bc, bs, 0, 1, 2)
+        dd[0, 1, 3] = product("dd", bc, bs, 0, 1, 3)
         scale_d(dd[0, 1, 0], 0, 1, 0)
         scale_d(dd[0, 1, 1], 0, 1, 1)
         scale_d(dd[0, 1, 2], 0, 1, 2)
         scale_d(dd[0, 1, 3], 0, 1, 3)
-        accum(mm[1, 1, 0], col_2, 1, 1, 0)
-        pre_be(1, 1, 0)
-        accum(mm[1, 1, 1], col_2, 1, 1, 1)
-        pre_be(1, 1, 1)
-        accum(mm[1, 1, 2], col_2, 1, 1, 2)
-        pre_be(1, 1, 2)
-        accum(mm[1, 1, 3], col_2, 1, 1, 3)
-        pre_be(1, 1, 3)
-        to[0, 0, 0] = turn_out(0, 0, 0, [True, True, True, True])
-        to[0, 0, 1] = turn_out(0, 0, 1, [True, True, True, True])
-        to[0, 0, 2] = turn_out(0, 0, 2, [True, True, True, True])
-        to[0, 0, 3] = turn_out(0, 0, 3, [True, True, True, True])
-        evac(to[0, 0, 0], 0, 0, 0, True)
-        evac(to[0, 0, 1], 0, 0, 1, True)
-        evac(to[0, 0, 2], 0, 0, 2, True)
-        evac(to[0, 0, 3], 0, 0, 3, True)
-        be[1, 0] = lay_be(1, 0)
-        be[1, 1] = lay_be(1, 1)
-        quant(bc[1, 0], bs[1, 0], be[1, 0])
+        add_qe(tqe[1, 0, 0], 1, 0, 0)
+        add_qe(tqe[1, 0, 1], 1, 0, 1)
+        mm[1, 0, 0] = product("mm", xc, xs, 1, 0, 0)
+        mm[1, 0, 1] = product("mm", xc, xs, 1, 0, 1)
+        mm[1, 0, 2] = product("mm", xc, xs, 1, 0, 2)
+        mm[1, 0, 3] = product("mm", xc, xs, 1, 0, 3)
+        accum(mm[1, 0, 0], col_2, 1, 0, 0)
+        accum(mm[1, 0, 1], col_2, 1, 0, 1)
+        accum(mm[1, 0, 2], col_2, 1, 0, 2)
+        accum(mm[1, 0, 3], col_2, 1, 0, 3)
+        pre_be(1, 1, 0, False)
+        pre_be(1, 1, 1, False)
+        pre_be(1, 1, 2, False)
+        pre_be(1, 1, 3, False)
+        pre_be(1, 0, 0, False)
+        pre_be(1, 0, 1, False)
+        pre_be(1, 0, 2, False)
+        pre_be(1, 0, 3, False)
+        be[1, 1] = lay_be(1, 1, True)
+        dd[0, 0, 0] = product("dd", bc, bs, 0, 0, 0)
+        dd[0, 0, 1] = product("dd", bc, bs, 0, 0, 1)
+        dd[0, 0, 2] = product("dd", bc, bs, 0, 0, 2)
+        dd[0, 0, 3] = product("dd", bc, bs, 0, 0, 3)
         to[0, 1, 0] = turn_out(0, 1, 0, [True, True, True, True])
         to[0, 1, 1] = turn_out(0, 1, 1, [True, True, True, True])
-        quant(bc[1, 1], bs[1, 1], be[1, 1])
-        dd[1, 0, 0] = product("dd", bc, bs, 1, 0, 0)
-        dd[1, 0, 1] = product("dd", bc, bs, 1, 0, 1)
-        dd[1, 0, 2] = product("dd", bc, bs, 1, 0, 2)
-        dd[1, 0, 3] = product("dd", bc, bs, 1, 0, 3)
         to[0, 1, 2] = turn_out(0, 1, 2, [True, True, True, True])
         to[0, 1, 3] = turn_out(0, 1, 3, [True, True, True, True])
+        accum(dd[0, 0, 0], col_1, 0, 0, 0)
+        scale_d(dd[0, 0, 1], 0, 0, 1)
+        accum(dd[0, 0, 2], col_1, 0, 0, 2)
+        scale_d(dd[0, 0, 3], 0, 0, 3)
+        be[1, 0] = lay_be(1, 0, False)
+        to[0, 0, 0] = turn_out(0, 0, 0, [False, True, False, True])
+        to[0, 0, 1] = turn_out(0, 0, 1, [False, True, False, True])
+        to[0, 0, 2] = turn_out(0, 0, 2, [False, True, False, True])
+        to[0, 0, 3] = turn_out(0, 0, 3, [False, True, False, True])
         evac(to[0, 1, 0], 0, 1, 0, True)
         evac(to[0, 1, 1], 0, 1, 1, True)
         evac(to[0, 1, 2], 0, 1, 2, True)
         evac(to[0, 1, 3], 0, 1, 3, True)
-        ob[0, 0] = cast_out(0, 0, False)
-        accum(dd[1, 0, 0], col_1, 1, 0, 0)
-        accum(dd[1, 0, 1], col_1, 1, 0, 1)
-        accum(dd[1, 0, 2], col_1, 1, 0, 2)
-        accum(dd[1, 0, 3], col_1, 1, 0, 3)
+        ob[0, 1] = cast_out(0, 1, True)
+        quant(bc[1, 1], bs[1, 1], be[1, 1])
+        quant(bc[1, 0], bs[1, 0], be[1, 0])
+        evac(to[0, 0, 0], 0, 0, 0, True)
+        evac(to[0, 0, 1], 0, 0, 1, False)
+        evac(to[0, 0, 2], 0, 0, 2, True)
+        evac(to[0, 0, 3], 0, 0, 3, False)
+        dd[1, 0, 0] = product("dd", bc, bs, 1, 0, 0)
+        dd[1, 0, 1] = product("dd", bc, bs, 1, 0, 1)
+        dd[1, 0, 2] = product("dd", bc, bs, 1, 0, 2)
+        dd[1, 0, 3] = product("dd", bc, bs, 1, 0, 3)
         dd[1, 1, 0] = product("dd", bc, bs, 1, 1, 0)
         dd[1, 1, 1] = product("dd", bc, bs, 1, 1, 1)
         dd[1, 1, 2] = product("dd", bc, bs, 1, 1, 2)
         dd[1, 1, 3] = product("dd", bc, bs, 1, 1, 3)
-        store_planes(ob[0, 0], 0, 0)
+        ob[0, 0] = cast_out(0, 0, True)
+        store_planes(ob[0, 1], 0, 1)
+        accum(dd[1, 0, 0], col_1, 1, 0, 0)
+        accum(dd[1, 0, 1], col_1, 1, 0, 1)
+        accum(dd[1, 0, 2], col_1, 1, 0, 2)
+        accum(dd[1, 0, 3], col_1, 1, 0, 3)
         to[1, 0, 0] = turn_out(1, 0, 0, [False, False, False, False])
         to[1, 0, 1] = turn_out(1, 0, 1, [False, False, False, False])
         to[1, 0, 2] = turn_out(1, 0, 2, [False, False, False, False])
         to[1, 0, 3] = turn_out(1, 0, 3, [False, False, False, False])
         scale_d(dd[1, 1, 0], 1, 1, 0)
-        scale_d(dd[1, 1, 1], 1, 1, 1)
+        accum(dd[1, 1, 1], col_1, 1, 1, 1)
         scale_d(dd[1, 1, 2], 1, 1, 2)
-        scale_d(dd[1, 1, 3], 1, 1, 3)
-        ob[0, 1] = cast_out(0, 1, False)
-        evac(to[1, 0, 0], 1, 0, 0, True)
+        accum(dd[1, 1, 3], col_1, 1, 1, 3)
+        store_planes(ob[0, 0], 0, 0)
+        to[1, 1, 0] = turn_out(1, 1, 0, [True, False, True, False])
+        to[1, 1, 1] = turn_out(1, 1, 1, [True, False, True, False])
+        to[1, 1, 2] = turn_out(1, 1, 2, [True, False, True, False])
+        to[1, 1, 3] = turn_out(1, 1, 3, [True, False, True, False])
+        evac(to[1, 0, 0], 1, 0, 0, False)
         evac(to[1, 0, 1], 1, 0, 1, True)
-        evac(to[1, 0, 2], 1, 0, 2, True)
+        evac(to[1, 0, 2], 1, 0, 2, False)
         evac(to[1, 0, 3], 1, 0, 3, True)
-        store_planes(ob[0, 1], 0, 1)
-        to[1, 1, 0] = turn_out(1, 1, 0, [True, True, True, True])
-        to[1, 1, 1] = turn_out(1, 1, 1, [True, True, True, True])
-        to[1, 1, 2] = turn_out(1, 1, 2, [True, True, True, True])
-        to[1, 1, 3] = turn_out(1, 1, 3, [True, True, True, True])
         evac(to[1, 1, 0], 1, 1, 0, False)
         evac(to[1, 1, 1], 1, 1, 1, True)
         evac(to[1, 1, 2], 1, 1, 2, False)
         evac(to[1, 1, 3], 1, 1, 3, True)
-        ob[1, 0] = cast_out(1, 0, False)
-        store_planes(ob[1, 0], 1, 0)
+        ob[1, 0] = cast_out(1, 0, True)
         ob[1, 1] = cast_out(1, 1, False)
         store_planes(ob[1, 1], 1, 1)
+        store_planes(ob[1, 0], 1, 0)

@@ -15,456 +15,347 @@ FP8X4 = mybir.dt.float8_e4m3fn_x4
 FP4X4 = mybir.dt.float4_e2m1fn_x4
 MULT = mybir.AluOpType.mult
 ADD = mybir.AluOpType.add
-SUB = mybir.AluOpType.subtract
 COPY = mybir.ActivationFunctionType.Copy
 
 P = 128
+PACK = 4
+GROUP = P * PACK
+N_CHUNKS = M // GROUP
+N_GROUPS = R // GROUP
+BANKS = 8
+
+GPSIMD_ADDS = {(1, 0)}
+GPSIMD_SCALES = {(0, 0), (1, 0)}
+VECTOR_CASTS = {(1, 1)}
+VECTOR_EMPTIES = {(0, 0): (1, 3), (0, 1): (), (1, 0): (0, 2), (1, 1): (1, 3)}
 
 
 def tile_muskingumnetworktwotermneumannrouting_x2_kernel(
     tc, q, qe, n_words, n_scales, e, c1, c2, out_0, out_1, out_2
 ):
     nc = tc.nc
+    units = [(c, g) for c in range(N_CHUNKS) for g in range(N_GROUPS)]
+
     with ExitStack() as ctx:
         keep = ctx.enter_context(tc.tile_pool(name="keep", bufs=1))
         work = ctx.enter_context(tc.tile_pool(name="work", bufs=2))
-        psum = ctx.enter_context(tc.psum_pool(name="psum", bufs=8))
+        psum = ctx.enter_context(tc.psum_pool(name="psum", bufs=BANKS))
         ctx.enter_context(tc.manual_schedule())
 
-        def kt(name, shape, dtype):
+        def kept(name, shape, dtype):
             return keep.tile(shape, dtype, name=name, tag=name, align_bytes=64)
 
-        def wt(name, shape, dtype, bufs):
+        def passing(name, shape, dtype, bufs):
             return work.tile(shape, dtype, name=name, tag=name, bufs=bufs, align_bytes=64)
 
-        ident = kt("ident", [P, P], F32)
-        vec_e = kt("vec_e", [P, 2, 4], BF16)
-        vec_1 = kt("vec_1", [P, 2, 4], BF16)
-        vec_2 = kt("vec_2", [P, 2, 4], BF16)
-        col_e = kt("col_e", [P, 2, 4], F32)
-        col_1 = kt("col_1", [P, 2, 4], F32)
-        col_2 = kt("col_2", [P, 2, 4], F32)
-        col_12 = kt("col_12", [P, 2, 4], F32)
-        col_3 = kt("col_3", [P, 2, 4], F32)
-        n_raw = kt("n_raw", [P, 2, 2048], U8)
-        n_per = kt("n_per", [P, 2, 2048], U8)
-        s_raw = kt("s_raw", [P, 2, 1024], U8)
-        s_per = kt("s_per", [P, 2, 1024], U8)
-        q_sb = [kt("q_sb%d" % G, [P, 4, R], BF16) for G in range(2)]
-        qe_sb = [kt("qe_sb%d" % G, [P, 4, R], BF16) for G in range(2)]
-        bb = {}
-        xc = {}
-        xs = {}
-        bc = {}
-        bs = {}
-        for G in range(2):
-            for g in range(2):
-                bb[G, g] = kt("bb%d%d" % (G, g), [P, 4, 512], F32)
-                xc[G, g] = kt("xc%d%d" % (G, g), [P, 512], U32)
-                xs[G, g] = kt("xs%d%d" % (G, g), [P, 512], U8)
-                bc[G, g] = kt("bc%d%d" % (G, g), [P, 512], U32)
-                bs[G, g] = kt("bs%d%d" % (G, g), [P, 512], U8)
+        def per_unit(name, shape, dtype):
+            return {(c, g): kept("%s_%d%d" % (name, c, g), shape, dtype) for c, g in units}
 
-        nc.gpsimd.memset(s_raw[:].rearrange("p g c -> p (g c)").bitcast(I32), 0)
+        identity = kept("identity", [P, P], F32)
+        e_bf16, c1_bf16, c2_bf16 = (kept(name, [P, N_GROUPS, PACK], BF16) for name in ("e_bf16", "c1_bf16", "c2_bf16"))
+        e_col, c1_col, c2_col = (kept(name, [P, N_GROUPS, PACK], F32) for name in ("e_col", "c1_col", "c2_col"))
+        c12_col = kept("c12_col", [P, N_GROUPS, PACK], F32)
+        c3_col = kept("c3_col", [P, N_GROUPS, PACK], F32)
+        words_in = kept("words_in", [P, N_GROUPS, 2 * R], U8)
+        words = kept("words", [P, N_GROUPS, 2 * R], U8)
+        scales_in = kept("scales_in", [P, N_GROUPS, R], U8)
+        scales = kept("scales", [P, N_GROUPS, R], U8)
+        q_rows = [kept("q_rows_%d" % c, [P, PACK, R], BF16) for c in range(N_CHUNKS)]
+        qe_rows = [kept("qe_rows_%d" % c, [P, PACK, R], BF16) for c in range(N_CHUNKS)]
+        b = per_unit("b", [P, PACK, GROUP], F32)
+        x_codes = per_unit("x_codes", [P, GROUP], U32)
+        x_scales = per_unit("x_scales", [P, GROUP], U8)
+        be_codes = per_unit("be_codes", [P, GROUP], U32)
+        be_scales = per_unit("be_scales", [P, GROUP], U8)
 
-        def load_rows(dst, src, G, tp):
-            rows = src[512 * G : 512 * G + 512, :].rearrange("(p t) k -> p t k", t=4)
-            nc.sync.dma_start(out=dst[G][:, 2 * tp : 2 * tp + 2, :], in_=rows[:, 2 * tp : 2 * tp + 2, :])
-
-        for src, dst in ((e, vec_e), (c1, vec_1), (c2, vec_2)):
-            nc.scalar.dma_start(out=dst[:], in_=src.rearrange("(g p t) -> p g t", g=2, t=4))
+        nc.gpsimd.memset(scales_in[:].rearrange("p g c -> p (g c)").bitcast(I32), 0)
+        for vector, tile in ((e, e_bf16), (c1, c1_bf16), (c2, c2_bf16)):
+            nc.scalar.dma_start(out=tile[:], in_=vector.rearrange("(g p t) -> p g t", g=N_GROUPS, t=PACK))
         for Q in range(4):
             nc.scalar.dma_start(
-                out=s_raw[32 * Q : 32 * Q + 4, :, :].bitcast(I32),
+                out=scales_in[32 * Q : 32 * Q + 4, :, :].bitcast(I32),
                 in_=n_scales[:, 4 * Q : 4 * Q + 4, :].rearrange("g q c -> q g c").bitcast(I32),
             )
-        for g in range(2):
-            nc.sync.dma_start(out=n_raw[:, g, :].bitcast(I32), in_=n_words[g].bitcast(I32))
-        load_rows(q_sb, q, 0, 0)
-        load_rows(q_sb, q, 0, 1)
-        load_rows(qe_sb, qe, 0, 0)
-        load_rows(qe_sb, qe, 0, 1)
-        load_rows(q_sb, q, 1, 0)
-        load_rows(q_sb, q, 1, 1)
-        load_rows(qe_sb, qe, 1, 0)
-        load_rows(qe_sb, qe, 1, 1)
+        for g in range(N_GROUPS):
+            nc.sync.dma_start(out=words_in[:, g, :].bitcast(I32), in_=n_words[g].bitcast(I32))
 
-        make_identity(nc, ident[:])
-        nc.gpsimd.tensor_tensor(out=col_12[:], in0=vec_1[:], in1=vec_2[:], op=ADD)
-        nc.gpsimd.tensor_scalar(out=col_3[:], in0=col_12[:], scalar1=-1.0, scalar2=1.0, op0=MULT, op1=ADD)
-        for col, vec in ((col_e, vec_e), (col_1, vec_1), (col_2, vec_2)):
-            nc.scalar.activation(out=col[:], in_=vec[:], func=COPY)
+        def of_chunk(dram, c):
+            return dram[GROUP * c : GROUP * (c + 1), :].rearrange("(p s) k -> p s k", s=PACK)
 
-        def permute_words(g, h):
-            nc.vector.tensor_copy(
-                out=n_per[:, g, 1024 * h : 1024 * h + 1024].rearrange("p (t m b) -> p t m b", t=4, b=2),
-                in_=n_raw[:, g, 1024 * h : 1024 * h + 1024].rearrange("p (m t b) -> p t m b", t=4, b=2),
-            )
+        for c in range(N_CHUNKS):
+            for dram, rows in ((q, q_rows), (qe, qe_rows)):
+                for s0 in (0, 2):
+                    nc.sync.dma_start(out=rows[c][:, s0 : s0 + 2, :], in_=of_chunk(dram, c)[:, s0 : s0 + 2, :])
 
-        def permute_scales(h):
-            nc.vector.tensor_copy(
-                out=s_per[:, :, 512 * h : 512 * h + 512].rearrange("p g (t m) -> p g t m", t=4),
-                in_=s_raw[:, :, 512 * h : 512 * h + 512].rearrange("p g (m t) -> p g t m", t=4),
-            )
+        make_identity(nc, identity[:])
+        nc.gpsimd.tensor_tensor(out=c12_col[:], in0=c1_bf16[:], in1=c2_bf16[:], op=ADD)
+        nc.gpsimd.tensor_scalar(out=c3_col[:], in0=c12_col[:], scalar1=-1.0, scalar2=1.0, op0=MULT, op1=ADD)
+        for col, tile in ((e_col, e_bf16), (c1_col, c1_bf16), (c2_col, c2_bf16)):
+            nc.scalar.activation(out=col[:], in_=tile[:], func=COPY)
 
-        def turn_q(G, tp, g):
-            bank = psum.tile([P, 2, 256], F32, name="bank", tag="bank", bufs=8)
-            for u in range(2):
-                for s in range(2):
-                    words = q_sb[G][:, 2 * tp + s, :].bitcast(F32)
-                    nc.tensor.transpose(
-                        bank[:, u, 128 * s : 128 * s + 128], words[:, 256 * g + u : 256 * g + 256 : 2], ident[:]
-                    )
-            return bank
-
-        def turn_qe(G, g, u):
-            bank = psum.tile([P, 512], F32, name="bank", tag="bank", bufs=8)
-            for s in range(4):
-                words = qe_sb[G][:, s, :].bitcast(F32)
-                nc.tensor.transpose(
-                    bank[:, 128 * s : 128 * s + 128], words[:, 256 * g + u : 256 * g + 256 : 2], ident[:]
+        def order_words(g):
+            cols = slice(2 * GROUP * g, 2 * GROUP * (g + 1))
+            for k in range(N_GROUPS):
+                nc.vector.tensor_copy(
+                    out=words[:, k, cols].rearrange("p (t m b) -> p t m b", t=PACK, b=2),
+                    in_=words_in[:, k, cols].rearrange("p (m t b) -> p t m b", t=PACK, b=2),
                 )
-            return bank
 
-        xb = {}
-
-        def make_x(bank, G, tp, g):
-            if (G, g) not in xb:
-                xb[G, g] = wt("xb", [P, 512, 4], BF16, 4)
-            nc.vector.tensor_tensor(
-                out=xb[G, g][:, 256 * tp : 256 * tp + 256, :].rearrange("p j (u w) -> p j u w", u=2),
-                in0=bank[:].bitcast(BF16).rearrange("p u (j w) -> p j u w", w=2),
-                in1=vec_e[:, g, :].rearrange("p (u w) -> p u w", u=2).unsqueeze(1).to_broadcast([P, 256, 2, 2]),
-                op=MULT,
+        def order_scales(g):
+            cols = slice(GROUP * g, GROUP * (g + 1))
+            nc.vector.tensor_copy(
+                out=scales[:, :, cols].rearrange("p k (t m) -> p k t m", t=PACK),
+                in_=scales_in[:, :, cols].rearrange("p k (m t) -> p k t m", t=PACK),
             )
 
-        def make_c3q(bank, G, tp, g):
-            view = bank[:].bitcast(BF16).rearrange("p u (j w) -> p u j w", w=2)
+        bank_of = {}
+
+        def turn(bank_part, rows, g, u):
+            nc.tensor.transpose(bank_part, rows.bitcast(F32)[:, GROUP // 2 * g + u : GROUP // 2 * (g + 1) : 2], identity[:])
+
+        def turn_q(c, half):
+            for g in range(N_GROUPS):
+                bank = psum.tile([P, 2, 2 * P], F32, name="bank", tag="bank", bufs=BANKS)
+                for u in range(2):
+                    for i in range(2):
+                        turn(bank[:, u, P * i : P * (i + 1)], q_rows[c][:, 2 * half + i, :], g, u)
+                bank_of["q", c, half, g] = bank
+
+        def turn_qe(c, g):
             for u in range(2):
-                for w in range(2):
-                    t = 2 * u + w
+                bank = psum.tile([P, GROUP], F32, name="bank", tag="bank", bufs=BANKS)
+                for s in range(PACK):
+                    turn(bank[:, P * s : P * (s + 1)], qe_rows[c][:, s, :], g, u)
+                bank_of["qe", c, g, u] = bank
+
+        x = {}
+
+        def make_x(c, half):
+            for g in range(N_GROUPS):
+                if half == 0:
+                    x[c, g] = passing("x", [P, GROUP, PACK], BF16, 4)
+                nc.vector.tensor_tensor(
+                    out=x[c, g][:, 2 * P * half : 2 * P * (half + 1), :].rearrange("p j (u w) -> p j u w", u=2),
+                    in0=bank_of["q", c, half, g][:].bitcast(BF16).rearrange("p u (j w) -> p j u w", w=2),
+                    in1=e_bf16[:, g, :].rearrange("p (u w) -> p u w", u=2).unsqueeze(1).to_broadcast([P, 2 * P, 2, 2]),
+                    op=MULT,
+                )
+
+        def quantise(codes, scale_bytes, values):
+            nc.vector.quantize_mx(
+                out=codes[:].bitcast(FP8X4), scales=scale_bytes[:], in_=values[:].rearrange("p j t -> p (j t)")
+            )
+
+        def quantise_x(c, g):
+            quantise(x_codes[c, g], x_scales[c, g], x[c, g])
+
+        def start_b(c, half):
+            for g in range(N_GROUPS):
+                slots = bank_of["q", c, half, g][:].bitcast(BF16).rearrange("p u (j w) -> p u j w", w=2)
+                for t in range(PACK):
                     nc.scalar.activation(
-                        out=bb[G, g][:, t, 256 * tp : 256 * tp + 256],
-                        in_=view[:, u, :, w],
+                        out=b[c, g][:, t, 2 * P * half : 2 * P * (half + 1)],
+                        in_=slots[:, t // 2, :, t % 2],
                         func=COPY,
-                        scale=col_3[:, g, t : t + 1],
+                        scale=c3_col[:, g, t : t + 1],
                     )
 
-        def quant(codes, scales, tile4):
-            nc.vector.quantize_mx(
-                out=codes[:].bitcast(FP8X4), scales=scales[:], in_=tile4[:].rearrange("p j t -> p (j t)")
-            )
+        qe_part = {}
 
-        def add_qe(bank, G, g, u):
-            view = bank[:].bitcast(BF16).rearrange("p (j w) -> p j w", w=2)
-            for w in range(2):
-                t = 2 * u + w
+        def add_qe(c, g):
+            for t in range(PACK):
+                slot = bank_of["qe", c, g, t // 2][:].bitcast(BF16).rearrange("p (j w) -> p j w", w=2)[:, :, t % 2]
+                weight = c12_col[:, g, t : t + 1]
+                if (c, g) not in GPSIMD_ADDS:
+                    nc.vector.scalar_tensor_tensor(
+                        out=b[c, g][:, t, :], in0=slot, scalar=weight, in1=b[c, g][:, t, :], op0=MULT, op1=ADD
+                    )
+                else:
+                    if t == 0:
+                        qe_part[c, g] = passing("qe_part", [P, PACK, GROUP], F32, 1)
+                    nc.scalar.activation(out=qe_part[c, g][:, t, :], in_=slot, func=COPY, scale=weight)
+
+        def add_qe_on_gpsimd(c, g):
+            for t in range(PACK):
+                nc.gpsimd.tensor_tensor(
+                    out=b[c, g][:, t, :], in0=qe_part[c, g][:, t, :], in1=b[c, g][:, t, :], op=ADD
+                )
+
+        def multiply(stage, codes, scale_bytes, c, g):
+            for t in range(PACK):
+                bank = psum.tile([P, GROUP], F32, name="bank", tag="bank", bufs=BANKS)
+                col = GROUP * g + P * t
+                for k in range(N_GROUPS):
+                    nc.tensor.matmul_mx(
+                        out=bank[:],
+                        lhsT=words[:, k, 2 * col : 2 * (col + P)].bitcast(FP4X4),
+                        lhsT_scale=scales[:, k, col : col + P],
+                        rhs=codes[c, k][:].bitcast(FP8X4),
+                        rhs_scale=scale_bytes[c, k][:],
+                        start=(k == 0),
+                        stop=(k == N_GROUPS - 1),
+                    )
+                bank_of[stage, c, g, t] = bank
+
+        def multiply_x(c, g):
+            multiply("a", x_codes, x_scales, c, g)
+
+        def multiply_be(c, g):
+            multiply("d", be_codes, be_scales, c, g)
+
+        def add_product(stage, col, c, g):
+            for t in range(PACK):
                 nc.vector.scalar_tensor_tensor(
-                    out=bb[G, g][:, t, :],
-                    in0=view[:, :, w],
-                    scalar=col_12[:, g, t : t + 1],
-                    in1=bb[G, g][:, t, :],
+                    out=b[c, g][:, t, :],
+                    in0=bank_of[stage, c, g, t][:],
+                    scalar=col[:, g, t : t + 1],
+                    in1=b[c, g][:, t, :],
                     op0=MULT,
                     op1=ADD,
                 )
 
-        def half_product(bank, codes, scales, G, g, t, k):
-            nc.tensor.matmul_mx(
-                out=bank[:],
-                lhsT=n_per[:, k, 1024 * g + 256 * t : 1024 * g + 256 * t + 256].bitcast(FP4X4),
-                lhsT_scale=s_per[:, k, 512 * g + 128 * t : 512 * g + 128 * t + 128],
-                rhs=codes[G, k][:].bitcast(FP8X4),
-                rhs_scale=scales[G, k][:],
-                start=(k == 0),
-                stop=(k == 1),
-            )
+        def finish_b(c, g):
+            add_product("a", c2_col, c, g)
 
-        def product(tag, codes, scales, G, g, t):
-            bank = psum.tile([P, 512], F32, name="bank", tag="bank", bufs=8)
-            for k in range(2):
-                half_product(bank, codes, scales, G, g, t, k)
-            return bank
+        def finish_out(c, g):
+            add_product("d", c1_col, c, g)
 
-        def accum(bank, col, G, g, t):
-            nc.vector.scalar_tensor_tensor(
-                out=bb[G, g][:, t, :],
-                in0=bank[:],
-                scalar=col[:, g, t : t + 1],
-                in1=bb[G, g][:, t, :],
-                op0=MULT,
-                op1=ADD,
-            )
-
-        def by_four(tile4):
-            return tile4[:].rearrange("p (c i) t -> p c t i", i=4)
-
-        eb = {}
-
-        def pre_be(G, g, t, on_scalar):
-            if t == 0:
-                eb[G, g] = wt("eb", [P, 4, 512], F32, 2)
-            if on_scalar:
-                nc.scalar.activation(
-                    out=eb[G, g][:, t, :], in_=bb[G, g][:, t, :], func=COPY, scale=col_e[:, g, t : t + 1]
-                )
-            else:
-                nc.gpsimd.tensor_scalar(
-                    out=eb[G, g][:, t, :], in0=bb[G, g][:, t, :], scalar1=col_e[:, g, t : t + 1],
-                    scalar2=0.0, op0=MULT, op1=ADD,
-                )
-
-        def lay_be(G, g, on_scalar):
-            tile4 = wt("be", [P, 512, 4], BF16, 4)
-            copy = nc.scalar.copy if on_scalar else nc.vector.tensor_copy
-            copy(out=by_four(tile4), in_=eb[G, g][:].rearrange("p t (c i) -> p c t i", i=4))
-            return tile4
-
-        cd = {}
-        of = {}
-        ob = {}
+        be_f32 = {}
         be = {}
-        to = {}
-        tq = {}
-        tqe = {}
-        mm = {}
-        dd = {}
 
-        def scale_d(bank, G, g, t):
-            if (G, g) not in cd:
-                cd[G, g] = wt("cd", [P, 4, 512], F32, 2)
-            nc.scalar.activation(out=cd[G, g][:, t, :], in_=bank[:], func=COPY, scale=col_1[:, g, t : t + 1])
+        def scale_b(c, g):
+            be_f32[c, g] = passing("be_f32", [P, PACK, GROUP], F32, 2)
+            for t in range(PACK):
+                src, dst, factor = b[c, g][:, t, :], be_f32[c, g][:, t, :], e_col[:, g, t : t + 1]
+                if (c, g) in GPSIMD_SCALES:
+                    nc.gpsimd.tensor_scalar(out=dst, in0=src, scalar1=factor, scalar2=0.0, op0=MULT, op1=ADD)
+                else:
+                    nc.scalar.activation(out=dst, in_=src, func=COPY, scale=factor)
 
-        def turn_out(G, g, s, by_pe):
-            bank = psum.tile([P, 4, P], F32, name="bank", tag="bank", bufs=8)
-            cols = slice(128 * s, 128 * s + 128)
-            for t in range(4):
-                nc.tensor.matmul(
-                    out=bank[:, t, :], lhsT=bb[G, g][:, t, cols], rhs=ident[:],
-                    start=True, stop=not by_pe[t], is_transpose=True,
+        def side_by_side(values):
+            return values[:].rearrange("p (j i) t -> p j t i", i=4)
+
+        def round_be(c, g):
+            be[c, g] = passing("be", [P, GROUP, PACK], BF16, 2)
+            nc.scalar.copy(out=side_by_side(be[c, g]), in_=be_f32[c, g][:].rearrange("p t (j i) -> p j t i", i=4))
+
+        def quantise_be(c, g):
+            quantise(be_codes[c, g], be_scales[c, g], be[c, g])
+
+        out_rows = {}
+        out_bf16 = {}
+
+        def turn_out(c, g):
+            for s in range(PACK):
+                bank = psum.tile([P, PACK, P], F32, name="bank", tag="bank", bufs=BANKS)
+                for t in range(PACK):
+                    nc.tensor.transpose(bank[:, t, :], b[c, g][:, t, P * s : P * (s + 1)], identity[:])
+                bank_of["out", c, g, s] = bank
+
+        def store_out(c, g, s0, s1):
+            rows = of_chunk(out_0, c)[:, :, GROUP * g : GROUP * (g + 1)]
+            nc.sync.dma_start(out=rows[:, s0:s1, :], in_=out_rows[c, g][:, s0:s1, :])
+
+        def empty_out(c, g):
+            out_rows[c, g] = passing("out_rows", [P, PACK, GROUP], F32, 4)
+            for s in range(PACK):
+                copy = nc.vector.tensor_copy if s in VECTOR_EMPTIES[c, g] else nc.scalar.copy
+                copy(
+                    out=out_rows[c, g][:, s, :].rearrange("p (r t) -> p r t", t=PACK),
+                    in_=bank_of["out", c, g, s][:].rearrange("p t r -> p r t"),
                 )
-                if by_pe[t]:
-                    nc.tensor.matmul(
-                        out=bank[:, t, :], lhsT=cd[G, g][:, t, cols], rhs=ident[:],
-                        start=False, stop=True, is_transpose=True,
-                    )
-            return bank
+                if s % 2 == 1:
+                    store_out(c, g, s - 1, s + 1)
 
-        def evac(bank, G, g, s, on_scalar):
-            if (G, g) not in of:
-                of[G, g] = wt("of", [P, 4, 512], F32, 4)
-            dst = of[G, g][:, s, :].rearrange("p (c t) -> p c t", t=4)
-            src = bank[:].rearrange("p t c -> p c t")
-            if on_scalar:
-                nc.scalar.copy(out=dst, in_=src)
-            else:
-                nc.vector.tensor_copy(out=dst, in_=src)
-            if (G, s) == (0, 3):
-                store_rows(G, g, 0, 4)
-            if G == 1 and s % 2 == 1:
-                store_rows(G, g, s - 1, s + 1)
+        def round_out(c, g):
+            out_bf16[c, g] = passing("out_bf16", [P, GROUP, PACK], BF16, 3)
+            copy = nc.vector.tensor_copy if (c, g) in VECTOR_CASTS else nc.scalar.copy
+            copy(out=side_by_side(out_bf16[c, g]), in_=out_rows[c, g][:].rearrange("p s (j i) -> p j s i", i=4))
 
-        def store_rows(G, g, s0, s1):
-            rows = out_0[512 * G : 512 * G + 512, 512 * g : 512 * g + 512].rearrange("(p t) r -> p t r", t=4)
-            nc.sync.dma_start(out=rows[:, s0:s1, :], in_=of[G, g][:, s0:s1, :])
-
-        def cast_out(G, g, on_scalar):
-            tile4 = wt("ob", [P, 512, 4], BF16, 2)
-            src = of[G, g][:].rearrange("p t (c i) -> p c t i", i=4)
-            if on_scalar:
-                nc.scalar.copy(out=by_four(tile4), in_=src)
-            else:
-                nc.vector.tensor_copy(out=by_four(tile4), in_=src)
-            return tile4
-
-        def store_planes(ob, G, g):
-            oc = wt("oc", [P, 512], U32, 4)
-            osc = wt("osc", [P, 512], U8, 4)
-            quant(oc, osc, ob)
+        def store_planes(c, g):
+            codes = passing("codes", [P, GROUP], U32, 4)
+            scale_bytes = passing("scale_bytes", [P, GROUP], U8, 4)
+            quantise(codes, scale_bytes, out_bf16[c, g])
+            cols = slice(GROUP * g, GROUP * (g + 1))
             nc.sync.dma_start(
-                out=out_1[G, :, 512 * g : 512 * g + 512, :].rearrange("p m t -> p (m t)").bitcast(I32),
-                in_=oc[:].bitcast(I32),
+                out=out_1[c, :, cols, :].rearrange("p r s -> p (r s)").bitcast(I32), in_=codes[:].bitcast(I32)
             )
+            queue = nc.scalar if c == N_CHUNKS - 1 else nc.sync
             for Q in range(4):
-                nc.sync.dma_start(
-                    out=out_2[G, 4 * Q : 4 * Q + 4, 512 * g : 512 * g + 512].bitcast(I32),
-                    in_=osc[32 * Q : 32 * Q + 4, :].bitcast(I32),
+                queue.dma_start(
+                    out=out_2[c, 4 * Q : 4 * Q + 4, cols].bitcast(I32), in_=scale_bytes[32 * Q : 32 * Q + 4, :].bitcast(I32)
                 )
 
-        permute_words(0, 0)
-        permute_words(1, 0)
-        tq[0, 0, 0] = turn_q(0, 0, 0)
-        tq[0, 0, 1] = turn_q(0, 0, 1)
-        permute_words(0, 1)
-        permute_words(1, 1)
-        make_x(tq[0, 0, 0], 0, 0, 0)
-        make_x(tq[0, 0, 1], 0, 0, 1)
-        make_c3q(tq[0, 0, 0], 0, 0, 0)
-        make_c3q(tq[0, 0, 1], 0, 0, 1)
-        tq[0, 1, 0] = turn_q(0, 1, 0)
-        tq[0, 1, 1] = turn_q(0, 1, 1)
-        tqe[0, 0, 0] = turn_qe(0, 0, 0)
-        tqe[0, 0, 1] = turn_qe(0, 0, 1)
-        make_x(tq[0, 1, 0], 0, 1, 0)
-        make_x(tq[0, 1, 1], 0, 1, 1)
-        tqe[0, 1, 0] = turn_qe(0, 1, 0)
-        tqe[0, 1, 1] = turn_qe(0, 1, 1)
-        permute_scales(0)
-        make_c3q(tq[0, 1, 0], 0, 1, 0)
-        make_c3q(tq[0, 1, 1], 0, 1, 1)
-        quant(xc[0, 0], xs[0, 0], xb[0, 0])
-        quant(xc[0, 1], xs[0, 1], xb[0, 1])
-        permute_scales(1)
-        tq[1, 0, 0] = turn_q(1, 0, 0)
-        tq[1, 0, 1] = turn_q(1, 0, 1)
-        add_qe(tqe[0, 0, 0], 0, 0, 0)
-        add_qe(tqe[0, 0, 1], 0, 0, 1)
-        tq[1, 1, 0] = turn_q(1, 1, 0)
-        tq[1, 1, 1] = turn_q(1, 1, 1)
-        add_qe(tqe[0, 1, 0], 0, 1, 0)
-        add_qe(tqe[0, 1, 1], 0, 1, 1)
-        make_c3q(tq[1, 1, 0], 1, 1, 0)
-        make_c3q(tq[1, 1, 1], 1, 1, 1)
-        mm[0, 1, 0] = product("mm", xc, xs, 0, 1, 0)
-        mm[0, 1, 1] = product("mm", xc, xs, 0, 1, 1)
-        mm[0, 1, 2] = product("mm", xc, xs, 0, 1, 2)
-        mm[0, 1, 3] = product("mm", xc, xs, 0, 1, 3)
-        accum(mm[0, 1, 0], col_2, 0, 1, 0)
-        accum(mm[0, 1, 1], col_2, 0, 1, 1)
-        accum(mm[0, 1, 2], col_2, 0, 1, 2)
-        accum(mm[0, 1, 3], col_2, 0, 1, 3)
-        make_c3q(tq[1, 0, 0], 1, 0, 0)
-        make_c3q(tq[1, 0, 1], 1, 0, 1)
-        mm[0, 0, 0] = product("mm", xc, xs, 0, 0, 0)
-        mm[0, 0, 1] = product("mm", xc, xs, 0, 0, 1)
-        mm[0, 0, 2] = product("mm", xc, xs, 0, 0, 2)
-        mm[0, 0, 3] = product("mm", xc, xs, 0, 0, 3)
-        accum(mm[0, 0, 0], col_2, 0, 0, 0)
-        accum(mm[0, 0, 1], col_2, 0, 0, 1)
-        accum(mm[0, 0, 2], col_2, 0, 0, 2)
-        accum(mm[0, 0, 3], col_2, 0, 0, 3)
-        tqe[1, 1, 0] = turn_qe(1, 1, 0)
-        tqe[1, 1, 1] = turn_qe(1, 1, 1)
-        pre_be(0, 1, 0, False)
-        pre_be(0, 1, 1, False)
-        pre_be(0, 1, 2, False)
-        pre_be(0, 1, 3, False)
-        be[0, 1] = lay_be(0, 1, True)
-        make_x(tq[1, 1, 0], 1, 1, 0)
-        make_x(tq[1, 1, 1], 1, 1, 1)
-        make_x(tq[1, 0, 0], 1, 0, 0)
-        make_x(tq[1, 0, 1], 1, 0, 1)
-        quant(bc[0, 1], bs[0, 1], be[0, 1])
-        tqe[1, 0, 0] = turn_qe(1, 0, 0)
-        tqe[1, 0, 1] = turn_qe(1, 0, 1)
-        quant(xc[1, 1], xs[1, 1], xb[1, 1])
-        pre_be(0, 0, 0, False)
-        pre_be(0, 0, 1, False)
-        pre_be(0, 0, 2, False)
-        pre_be(0, 0, 3, False)
-        quant(xc[1, 0], xs[1, 0], xb[1, 0])
-        be[0, 0] = lay_be(0, 0, True)
-        quant(bc[0, 0], bs[0, 0], be[0, 0])
-        add_qe(tqe[1, 1, 0], 1, 1, 0)
-        add_qe(tqe[1, 1, 1], 1, 1, 1)
-        mm[1, 1, 0] = product("mm", xc, xs, 1, 1, 0)
-        mm[1, 1, 1] = product("mm", xc, xs, 1, 1, 1)
-        mm[1, 1, 2] = product("mm", xc, xs, 1, 1, 2)
-        mm[1, 1, 3] = product("mm", xc, xs, 1, 1, 3)
-        accum(mm[1, 1, 0], col_2, 1, 1, 0)
-        accum(mm[1, 1, 1], col_2, 1, 1, 1)
-        accum(mm[1, 1, 2], col_2, 1, 1, 2)
-        accum(mm[1, 1, 3], col_2, 1, 1, 3)
-        dd[0, 1, 0] = product("dd", bc, bs, 0, 1, 0)
-        dd[0, 1, 1] = product("dd", bc, bs, 0, 1, 1)
-        dd[0, 1, 2] = product("dd", bc, bs, 0, 1, 2)
-        dd[0, 1, 3] = product("dd", bc, bs, 0, 1, 3)
-        scale_d(dd[0, 1, 0], 0, 1, 0)
-        scale_d(dd[0, 1, 1], 0, 1, 1)
-        scale_d(dd[0, 1, 2], 0, 1, 2)
-        scale_d(dd[0, 1, 3], 0, 1, 3)
-        add_qe(tqe[1, 0, 0], 1, 0, 0)
-        add_qe(tqe[1, 0, 1], 1, 0, 1)
-        mm[1, 0, 0] = product("mm", xc, xs, 1, 0, 0)
-        mm[1, 0, 1] = product("mm", xc, xs, 1, 0, 1)
-        mm[1, 0, 2] = product("mm", xc, xs, 1, 0, 2)
-        mm[1, 0, 3] = product("mm", xc, xs, 1, 0, 3)
-        accum(mm[1, 0, 0], col_2, 1, 0, 0)
-        accum(mm[1, 0, 1], col_2, 1, 0, 1)
-        accum(mm[1, 0, 2], col_2, 1, 0, 2)
-        accum(mm[1, 0, 3], col_2, 1, 0, 3)
-        pre_be(1, 1, 0, False)
-        pre_be(1, 1, 1, False)
-        pre_be(1, 1, 2, False)
-        pre_be(1, 1, 3, False)
-        pre_be(1, 0, 0, False)
-        pre_be(1, 0, 1, False)
-        pre_be(1, 0, 2, False)
-        pre_be(1, 0, 3, False)
-        be[1, 1] = lay_be(1, 1, True)
-        dd[0, 0, 0] = product("dd", bc, bs, 0, 0, 0)
-        dd[0, 0, 1] = product("dd", bc, bs, 0, 0, 1)
-        dd[0, 0, 2] = product("dd", bc, bs, 0, 0, 2)
-        dd[0, 0, 3] = product("dd", bc, bs, 0, 0, 3)
-        to[0, 1, 0] = turn_out(0, 1, 0, [True, True, True, True])
-        to[0, 1, 1] = turn_out(0, 1, 1, [True, True, True, True])
-        to[0, 1, 2] = turn_out(0, 1, 2, [True, True, True, True])
-        to[0, 1, 3] = turn_out(0, 1, 3, [True, True, True, True])
-        accum(dd[0, 0, 0], col_1, 0, 0, 0)
-        scale_d(dd[0, 0, 1], 0, 0, 1)
-        accum(dd[0, 0, 2], col_1, 0, 0, 2)
-        scale_d(dd[0, 0, 3], 0, 0, 3)
-        be[1, 0] = lay_be(1, 0, False)
-        to[0, 0, 0] = turn_out(0, 0, 0, [False, True, False, True])
-        to[0, 0, 1] = turn_out(0, 0, 1, [False, True, False, True])
-        to[0, 0, 2] = turn_out(0, 0, 2, [False, True, False, True])
-        to[0, 0, 3] = turn_out(0, 0, 3, [False, True, False, True])
-        evac(to[0, 1, 0], 0, 1, 0, True)
-        evac(to[0, 1, 1], 0, 1, 1, True)
-        evac(to[0, 1, 2], 0, 1, 2, True)
-        evac(to[0, 1, 3], 0, 1, 3, True)
-        ob[0, 1] = cast_out(0, 1, True)
-        quant(bc[1, 1], bs[1, 1], be[1, 1])
-        quant(bc[1, 0], bs[1, 0], be[1, 0])
-        evac(to[0, 0, 0], 0, 0, 0, True)
-        evac(to[0, 0, 1], 0, 0, 1, False)
-        evac(to[0, 0, 2], 0, 0, 2, True)
-        evac(to[0, 0, 3], 0, 0, 3, False)
-        dd[1, 0, 0] = product("dd", bc, bs, 1, 0, 0)
-        dd[1, 0, 1] = product("dd", bc, bs, 1, 0, 1)
-        dd[1, 0, 2] = product("dd", bc, bs, 1, 0, 2)
-        dd[1, 0, 3] = product("dd", bc, bs, 1, 0, 3)
-        dd[1, 1, 0] = product("dd", bc, bs, 1, 1, 0)
-        dd[1, 1, 1] = product("dd", bc, bs, 1, 1, 1)
-        dd[1, 1, 2] = product("dd", bc, bs, 1, 1, 2)
-        dd[1, 1, 3] = product("dd", bc, bs, 1, 1, 3)
-        ob[0, 0] = cast_out(0, 0, True)
-        store_planes(ob[0, 1], 0, 1)
-        accum(dd[1, 0, 0], col_1, 1, 0, 0)
-        accum(dd[1, 0, 1], col_1, 1, 0, 1)
-        accum(dd[1, 0, 2], col_1, 1, 0, 2)
-        accum(dd[1, 0, 3], col_1, 1, 0, 3)
-        to[1, 0, 0] = turn_out(1, 0, 0, [False, False, False, False])
-        to[1, 0, 1] = turn_out(1, 0, 1, [False, False, False, False])
-        to[1, 0, 2] = turn_out(1, 0, 2, [False, False, False, False])
-        to[1, 0, 3] = turn_out(1, 0, 3, [False, False, False, False])
-        scale_d(dd[1, 1, 0], 1, 1, 0)
-        accum(dd[1, 1, 1], col_1, 1, 1, 1)
-        scale_d(dd[1, 1, 2], 1, 1, 2)
-        accum(dd[1, 1, 3], col_1, 1, 1, 3)
-        store_planes(ob[0, 0], 0, 0)
-        to[1, 1, 0] = turn_out(1, 1, 0, [True, False, True, False])
-        to[1, 1, 1] = turn_out(1, 1, 1, [True, False, True, False])
-        to[1, 1, 2] = turn_out(1, 1, 2, [True, False, True, False])
-        to[1, 1, 3] = turn_out(1, 1, 3, [True, False, True, False])
-        evac(to[1, 0, 0], 1, 0, 0, False)
-        evac(to[1, 0, 1], 1, 0, 1, True)
-        evac(to[1, 0, 2], 1, 0, 2, False)
-        evac(to[1, 0, 3], 1, 0, 3, True)
-        evac(to[1, 1, 0], 1, 1, 0, False)
-        evac(to[1, 1, 1], 1, 1, 1, True)
-        evac(to[1, 1, 2], 1, 1, 2, False)
-        evac(to[1, 1, 3], 1, 1, 3, True)
-        ob[1, 0] = cast_out(1, 0, True)
-        ob[1, 1] = cast_out(1, 1, False)
-        store_planes(ob[1, 1], 1, 1)
-        store_planes(ob[1, 0], 1, 0)
+        order_words(0)
+        order_words(1)
+        turn_q(0, 0)
+        make_x(0, 0)
+        turn_q(0, 1)
+        start_b(0, 0)
+        make_x(0, 1)
+        turn_q(1, 0)
+        start_b(0, 1)
+        quantise_x(0, 0)
+        order_scales(0)
+        quantise_x(0, 1)
+        make_x(1, 0)
+        turn_q(1, 1)
+        make_x(1, 1)
+        start_b(1, 0)
+        turn_qe(0, 0)
+        turn_qe(0, 1)
+        start_b(1, 1)
+        order_scales(1)
+        add_qe(0, 0)
+        multiply_x(0, 0)
+        finish_b(0, 0)
+        turn_qe(1, 0)
+        quantise_x(1, 0)
+        quantise_x(1, 1)
+        add_qe(0, 1)
+        scale_b(0, 0)
+        add_qe(1, 0)
+        round_be(0, 0)
+        multiply_x(0, 1)
+        finish_b(0, 1)
+        scale_b(0, 1)
+        turn_qe(1, 1)
+        round_be(0, 1)
+        add_qe(1, 1)
+        add_qe_on_gpsimd(1, 0)
+        multiply_x(1, 1)
+        quantise_be(0, 0)
+        multiply_x(1, 0)
+        finish_b(1, 1)
+        scale_b(1, 1)
+        round_be(1, 1)
+        quantise_be(0, 1)
+        finish_b(1, 0)
+        scale_b(1, 0)
+        multiply_be(0, 0)
+        multiply_be(0, 1)
+        round_be(1, 0)
+        finish_out(0, 0)
+        finish_out(0, 1)
+        turn_out(0, 0)
+        quantise_be(1, 1)
+        turn_out(0, 1)
+        quantise_be(1, 0)
+        empty_out(0, 0)
+        empty_out(0, 1)
+        multiply_be(1, 0)
+        finish_out(1, 0)
+        multiply_be(1, 1)
+        finish_out(1, 1)
+        turn_out(1, 0)
+        round_out(0, 0)
+        store_planes(0, 0)
+        turn_out(1, 1)
+        round_out(0, 1)
+        empty_out(1, 0)
+        empty_out(1, 1)
+        store_planes(0, 1)
+        round_out(1, 1)
+        round_out(1, 0)
+        store_planes(1, 0)
+        store_planes(1, 1)

@@ -26,8 +26,8 @@ BANKS = 8
 
 GPSIMD_ADDS = {(1, 0)}
 GPSIMD_SCALES = {(0, 0), (1, 0)}
-VECTOR_CASTS = {(1, 1)}
-VECTOR_EMPTIES = {(0, 0): (1, 3), (0, 1): (), (1, 0): (0, 2), (1, 1): (1, 3)}
+VECTOR_CASTS = {(0, 1), (1, 0)}
+VECTOR_EMPTIES = {(0, 0): (), (0, 1): (1, 3), (1, 0): (), (1, 1): (0, 2)}
 
 
 def tile_muskingumnetworktwotermneumannrouting_x2_kernel(
@@ -220,13 +220,13 @@ def tile_muskingumnetworktwotermneumannrouting_x2_kernel(
         def finish_out(c, g):
             add_product("d", c1_col, c, g)
 
-        be_f32 = {}
+        be_slots = {}
         be = {}
 
         def scale_b(c, g):
-            be_f32[c, g] = passing("be_f32", [P, PACK, GROUP], F32, 2)
+            be_slots[c, g] = passing("be_slots", [P, PACK, GROUP], BF16, 2)
             for t in range(PACK):
-                src, dst, factor = b[c, g][:, t, :], be_f32[c, g][:, t, :], e_col[:, g, t : t + 1]
+                src, dst, factor = b[c, g][:, t, :], be_slots[c, g][:, t, :], e_col[:, g, t : t + 1]
                 if (c, g) in GPSIMD_SCALES:
                     nc.gpsimd.tensor_scalar(out=dst, in0=src, scalar1=factor, scalar2=0.0, op0=MULT, op1=ADD)
                 else:
@@ -235,9 +235,9 @@ def tile_muskingumnetworktwotermneumannrouting_x2_kernel(
         def side_by_side(values):
             return values[:].rearrange("p (j i) t -> p j t i", i=4)
 
-        def round_be(c, g):
+        def pack_be(c, g):
             be[c, g] = passing("be", [P, GROUP, PACK], BF16, 2)
-            nc.scalar.copy(out=side_by_side(be[c, g]), in_=be_f32[c, g][:].rearrange("p t (j i) -> p j t i", i=4))
+            nc.scalar.copy(out=side_by_side(be[c, g]), in_=be_slots[c, g][:].rearrange("p t (j i) -> p j t i", i=4))
 
         def quantise_be(c, g):
             quantise(be_codes[c, g], be_scales[c, g], be[c, g])
@@ -286,76 +286,76 @@ def tile_muskingumnetworktwotermneumannrouting_x2_kernel(
                     out=out_2[c, 4 * Q : 4 * Q + 4, cols].bitcast(I32), in_=scale_bytes[32 * Q : 32 * Q + 4, :].bitcast(I32)
                 )
 
+        turn_q(0, 0)
+        turn_q(0, 1)
         order_words(0)
         order_words(1)
-        turn_q(0, 0)
         make_x(0, 0)
-        turn_q(0, 1)
-        start_b(0, 0)
-        make_x(0, 1)
+        turn_qe(0, 0)
         turn_q(1, 0)
+        make_x(0, 1)
+        order_scales(0)
+        start_b(0, 0)
+        turn_q(1, 1)
         start_b(0, 1)
         quantise_x(0, 0)
-        order_scales(0)
         quantise_x(0, 1)
-        make_x(1, 0)
-        turn_q(1, 1)
-        make_x(1, 1)
-        start_b(1, 0)
-        turn_qe(0, 0)
-        turn_qe(0, 1)
-        start_b(1, 1)
         order_scales(1)
+        make_x(1, 0)
         add_qe(0, 0)
+        start_b(1, 0)
         multiply_x(0, 0)
         finish_b(0, 0)
+        start_b(1, 1)
+        make_x(1, 1)
         turn_qe(1, 0)
-        quantise_x(1, 0)
-        quantise_x(1, 1)
-        add_qe(0, 1)
-        scale_b(0, 0)
         add_qe(1, 0)
-        round_be(0, 0)
+        turn_qe(0, 1)
+        scale_b(0, 0)
+        add_qe(0, 1)
         multiply_x(0, 1)
-        finish_b(0, 1)
-        scale_b(0, 1)
         turn_qe(1, 1)
-        round_be(0, 1)
+        finish_b(0, 1)
+        pack_be(0, 0)
+        quantise_x(1, 0)
+        quantise_be(0, 0)
+        quantise_x(1, 1)
+        multiply_x(1, 1)
         add_qe(1, 1)
         add_qe_on_gpsimd(1, 0)
-        multiply_x(1, 1)
-        quantise_be(0, 0)
-        multiply_x(1, 0)
         finish_b(1, 1)
-        scale_b(1, 1)
-        round_be(1, 1)
+        scale_b(0, 1)
+        multiply_x(1, 0)
+        pack_be(0, 1)
         quantise_be(0, 1)
         finish_b(1, 0)
-        scale_b(1, 0)
         multiply_be(0, 0)
-        multiply_be(0, 1)
-        round_be(1, 0)
+        scale_b(1, 1)
+        scale_b(1, 0)
         finish_out(0, 0)
+        pack_be(1, 1)
+        pack_be(1, 0)
+        multiply_be(0, 1)
         finish_out(0, 1)
-        turn_out(0, 0)
         quantise_be(1, 1)
-        turn_out(0, 1)
         quantise_be(1, 0)
+        turn_out(0, 0)
         empty_out(0, 0)
+        turn_out(0, 1)
         empty_out(0, 1)
         multiply_be(1, 0)
         finish_out(1, 0)
         multiply_be(1, 1)
+        round_out(0, 0)
         finish_out(1, 1)
         turn_out(1, 0)
-        round_out(0, 0)
-        store_planes(0, 0)
-        turn_out(1, 1)
-        round_out(0, 1)
         empty_out(1, 0)
+        round_out(0, 1)
+        turn_out(1, 1)
         empty_out(1, 1)
         store_planes(0, 1)
         round_out(1, 1)
+        store_planes(0, 0)
         round_out(1, 0)
         store_planes(1, 0)
         store_planes(1, 1)

from contextlib import ExitStack

import concourse.mybir as mybir
from concourse.masks import make_identity

M, R = 1024, 1024
FLOPS = 2 * 2 * M * R * R

F32 = mybir.dt.float32
BF16 = mybir.dt.bfloat16
I32 = mybir.dt.int32
U32 = mybir.dt.uint32
U8 = mybir.dt.uint8
FP8X4 = mybir.dt.float8_e4m3fn_x4
FP4X4 = mybir.dt.float4_e2m1fn_x4
MULT = mybir.AluOpType.mult
ADD = mybir.AluOpType.add
COPY = mybir.ActivationFunctionType.Copy

P = 128
PACK = 4
GROUP = P * PACK
N_CHUNKS = M // GROUP
N_GROUPS = R // GROUP
BANKS = 8

GPSIMD_ADDS = {(1, 0)}
GPSIMD_SCALES = {(0, 0), (1, 0)}
VECTOR_CASTS = {(0, 1), (1, 0)}
VECTOR_EMPTIES = {(0, 0): (), (0, 1): (1, 3), (1, 0): (), (1, 1): (0, 2)}


def tile_muskingumnetworktwotermneumannrouting_x2_kernel(
    tc, q, qe, n_words, n_scales, e, c1, c2, out_0, out_1, out_2
):
    nc = tc.nc
    units = [(c, g) for c in range(N_CHUNKS) for g in range(N_GROUPS)]

    with ExitStack() as ctx:
        keep = ctx.enter_context(tc.tile_pool(name="keep", bufs=1))
        work = ctx.enter_context(tc.tile_pool(name="work", bufs=2))
        psum = ctx.enter_context(tc.psum_pool(name="psum", bufs=BANKS))
        ctx.enter_context(tc.manual_schedule())

        def kept(name, shape, dtype):
            return keep.tile(shape, dtype, name=name, tag=name, align_bytes=64)

        def passing(name, shape, dtype, bufs):
            return work.tile(shape, dtype, name=name, tag=name, bufs=bufs, align_bytes=64)

        def per_unit(name, shape, dtype):
            return {(c, g): kept("%s_%d%d" % (name, c, g), shape, dtype) for c, g in units}

        identity = kept("identity", [P, P], F32)
        e_bf16, c1_bf16, c2_bf16 = (kept(name, [P, N_GROUPS, PACK], BF16) for name in ("e_bf16", "c1_bf16", "c2_bf16"))
        e_col, c1_col, c2_col = (kept(name, [P, N_GROUPS, PACK], F32) for name in ("e_col", "c1_col", "c2_col"))
        c12_col = kept("c12_col", [P, N_GROUPS, PACK], F32)
        c3_col = kept("c3_col", [P, N_GROUPS, PACK], F32)
        words_in = kept("words_in", [P, N_GROUPS, 2 * R], U8)
        words = kept("words", [P, N_GROUPS, 2 * R], U8)
        scales_in = kept("scales_in", [P, N_GROUPS, R], U8)
        scales = kept("scales", [P, N_GROUPS, R], U8)
        q_rows = [kept("q_rows_%d" % c, [P, PACK, R], BF16) for c in range(N_CHUNKS)]
        qe_rows = [kept("qe_rows_%d" % c, [P, PACK, R], BF16) for c in range(N_CHUNKS)]
        b = per_unit("b", [P, PACK, GROUP], F32)
        x_codes = per_unit("x_codes", [P, GROUP], U32)
        x_scales = per_unit("x_scales", [P, GROUP], U8)
        be_codes = per_unit("be_codes", [P, GROUP], U32)
        be_scales = per_unit("be_scales", [P, GROUP], U8)

        nc.gpsimd.memset(scales_in[:].rearrange("p g c -> p (g c)").bitcast(I32), 0)
        for vector, tile in ((e, e_bf16), (c1, c1_bf16), (c2, c2_bf16)):
            nc.scalar.dma_start(out=tile[:], in_=vector.rearrange("(g p t) -> p g t", g=N_GROUPS, t=PACK))
        for Q in range(4):
            nc.scalar.dma_start(
                out=scales_in[32 * Q : 32 * Q + 4, :, :].bitcast(I32),
                in_=n_scales[:, 4 * Q : 4 * Q + 4, :].rearrange("g q c -> q g c").bitcast(I32),
            )
        for g in range(N_GROUPS):
            nc.sync.dma_start(out=words_in[:, g, :].bitcast(I32), in_=n_words[g].bitcast(I32))

        def of_chunk(dram, c):
            return dram[GROUP * c : GROUP * (c + 1), :].rearrange("(p s) k -> p s k", s=PACK)

        for c in range(N_CHUNKS):
            for dram, rows in ((q, q_rows), (qe, qe_rows)):
                for s0 in (0, 2):
                    nc.sync.dma_start(out=rows[c][:, s0 : s0 + 2, :], in_=of_chunk(dram, c)[:, s0 : s0 + 2, :])

        make_identity(nc, identity[:])
        nc.gpsimd.tensor_tensor(out=c12_col[:], in0=c1_bf16[:], in1=c2_bf16[:], op=ADD)
        nc.gpsimd.tensor_scalar(out=c3_col[:], in0=c12_col[:], scalar1=-1.0, scalar2=1.0, op0=MULT, op1=ADD)
        for col, tile in ((e_col, e_bf16), (c1_col, c1_bf16), (c2_col, c2_bf16)):
            nc.scalar.activation(out=col[:], in_=tile[:], func=COPY)

        def order_words(g):
            cols = slice(2 * GROUP * g, 2 * GROUP * (g + 1))
            for k in range(N_GROUPS):
                nc.vector.tensor_copy(
                    out=words[:, k, cols].rearrange("p (t m b) -> p t m b", t=PACK, b=2),
                    in_=words_in[:, k, cols].rearrange("p (m t b) -> p t m b", t=PACK, b=2),
                )

        def order_scales(g):
            cols = slice(GROUP * g, GROUP * (g + 1))
            nc.vector.tensor_copy(
                out=scales[:, :, cols].rearrange("p k (t m) -> p k t m", t=PACK),
                in_=scales_in[:, :, cols].rearrange("p k (m t) -> p k t m", t=PACK),
            )

        bank_of = {}

        def turn(bank_part, rows, g, u):
            nc.tensor.transpose(bank_part, rows.bitcast(F32)[:, GROUP // 2 * g + u : GROUP // 2 * (g + 1) : 2], identity[:])

        def turn_q(c, half):
            for g in range(N_GROUPS):
                bank = psum.tile([P, 2, 2 * P], F32, name="bank", tag="bank", bufs=BANKS)
                for u in range(2):
                    for i in range(2):
                        turn(bank[:, u, P * i : P * (i + 1)], q_rows[c][:, 2 * half + i, :], g, u)
                bank_of["q", c, half, g] = bank

        def turn_qe(c, g):
            for u in range(2):
                bank = psum.tile([P, GROUP], F32, name="bank", tag="bank", bufs=BANKS)
                for s in range(PACK):
                    turn(bank[:, P * s : P * (s + 1)], qe_rows[c][:, s, :], g, u)
                bank_of["qe", c, g, u] = bank

        x = {}

        def make_x(c, half):
            for g in range(N_GROUPS):
                if half == 0:
                    x[c, g] = passing("x", [P, GROUP, PACK], BF16, 4)
                nc.vector.tensor_tensor(
                    out=x[c, g][:, 2 * P * half : 2 * P * (half + 1), :].rearrange("p j (u w) -> p j u w", u=2),
                    in0=bank_of["q", c, half, g][:].bitcast(BF16).rearrange("p u (j w) -> p j u w", w=2),
                    in1=e_bf16[:, g, :].rearrange("p (u w) -> p u w", u=2).unsqueeze(1).to_broadcast([P, 2 * P, 2, 2]),
                    op=MULT,
                )

        def quantise(codes, scale_bytes, values):
            nc.vector.quantize_mx(
                out=codes[:].bitcast(FP8X4), scales=scale_bytes[:], in_=values[:].rearrange("p j t -> p (j t)")
            )

        def quantise_x(c, g):
            quantise(x_codes[c, g], x_scales[c, g], x[c, g])

        def start_b(c, half):
            for g in range(N_GROUPS):
                slots = bank_of["q", c, half, g][:].bitcast(BF16).rearrange("p u (j w) -> p u j w", w=2)
                for t in range(PACK):
                    nc.scalar.activation(
                        out=b[c, g][:, t, 2 * P * half : 2 * P * (half + 1)],
                        in_=slots[:, t // 2, :, t % 2],
                        func=COPY,
                        scale=c3_col[:, g, t : t + 1],
                    )

        qe_part = {}

        def add_qe(c, g):
            for t in range(PACK):
                slot = bank_of["qe", c, g, t // 2][:].bitcast(BF16).rearrange("p (j w) -> p j w", w=2)[:, :, t % 2]
                weight = c12_col[:, g, t : t + 1]
                if (c, g) not in GPSIMD_ADDS:
                    nc.vector.scalar_tensor_tensor(
                        out=b[c, g][:, t, :], in0=slot, scalar=weight, in1=b[c, g][:, t, :], op0=MULT, op1=ADD
                    )
                else:
                    if t == 0:
                        qe_part[c, g] = passing("qe_part", [P, PACK, GROUP], F32, 1)
                    nc.scalar.activation(out=qe_part[c, g][:, t, :], in_=slot, func=COPY, scale=weight)

        def add_qe_on_gpsimd(c, g):
            for t in range(PACK):
                nc.gpsimd.tensor_tensor(
                    out=b[c, g][:, t, :], in0=qe_part[c, g][:, t, :], in1=b[c, g][:, t, :], op=ADD
                )

        def multiply(stage, codes, scale_bytes, c, g):
            for t in range(PACK):
                bank = psum.tile([P, GROUP], F32, name="bank", tag="bank", bufs=BANKS)
                col = GROUP * g + P * t
                for k in range(N_GROUPS):
                    nc.tensor.matmul_mx(
                        out=bank[:],
                        lhsT=words[:, k, 2 * col : 2 * (col + P)].bitcast(FP4X4),
                        lhsT_scale=scales[:, k, col : col + P],
                        rhs=codes[c, k][:].bitcast(FP8X4),
                        rhs_scale=scale_bytes[c, k][:],
                        start=(k == 0),
                        stop=(k == N_GROUPS - 1),
                    )
                bank_of[stage, c, g, t] = bank

        def multiply_x(c, g):
            multiply("a", x_codes, x_scales, c, g)

        def multiply_be(c, g):
            multiply("d", be_codes, be_scales, c, g)

        def add_product(stage, col, c, g):
            for t in range(PACK):
                nc.vector.scalar_tensor_tensor(
                    out=b[c, g][:, t, :],
                    in0=bank_of[stage, c, g, t][:],
                    scalar=col[:, g, t : t + 1],
                    in1=b[c, g][:, t, :],
                    op0=MULT,
                    op1=ADD,
                )

        def finish_b(c, g):
            add_product("a", c2_col, c, g)

        def finish_out(c, g):
            add_product("d", c1_col, c, g)

        be_slots = {}
        be = {}

        def scale_b(c, g):
            be_slots[c, g] = passing("be_slots", [P, PACK, GROUP], BF16, 2)
            for t in range(PACK):
                src, dst, factor = b[c, g][:, t, :], be_slots[c, g][:, t, :], e_col[:, g, t : t + 1]
                if (c, g) in GPSIMD_SCALES:
                    nc.gpsimd.tensor_scalar(out=dst, in0=src, scalar1=factor, scalar2=0.0, op0=MULT, op1=ADD)
                else:
                    nc.scalar.activation(out=dst, in_=src, func=COPY, scale=factor)

        def side_by_side(values):
            return values[:].rearrange("p (j i) t -> p j t i", i=4)

        def pack_be(c, g):
            be[c, g] = passing("be", [P, GROUP, PACK], BF16, 2)
            nc.scalar.copy(out=side_by_side(be[c, g]), in_=be_slots[c, g][:].rearrange("p t (j i) -> p j t i", i=4))

        def quantise_be(c, g):
            quantise(be_codes[c, g], be_scales[c, g], be[c, g])

        out_rows = {}
        out_bf16 = {}

        def turn_out(c, g):
            for s in range(PACK):
                bank = psum.tile([P, PACK, P], F32, name="bank", tag="bank", bufs=BANKS)
                for t in range(PACK):
                    nc.tensor.transpose(bank[:, t, :], b[c, g][:, t, P * s : P * (s + 1)], identity[:])
                bank_of["out", c, g, s] = bank

        def store_out(c, g, s0, s1):
            rows = of_chunk(out_0, c)[:, :, GROUP * g : GROUP * (g + 1)]
            nc.sync.dma_start(out=rows[:, s0:s1, :], in_=out_rows[c, g][:, s0:s1, :])

        def empty_out(c, g):
            out_rows[c, g] = passing("out_rows", [P, PACK, GROUP], F32, 4)
            for s in range(PACK):
                copy = nc.vector.tensor_copy if s in VECTOR_EMPTIES[c, g] else nc.scalar.copy
                copy(
                    out=out_rows[c, g][:, s, :].rearrange("p (r t) -> p r t", t=PACK),
                    in_=bank_of["out", c, g, s][:].rearrange("p t r -> p r t"),
                )
                if s % 2 == 1:
                    store_out(c, g, s - 1, s + 1)

        def round_out(c, g):
            out_bf16[c, g] = passing("out_bf16", [P, GROUP, PACK], BF16, 3)
            copy = nc.vector.tensor_copy if (c, g) in VECTOR_CASTS else nc.scalar.copy
            copy(out=side_by_side(out_bf16[c, g]), in_=out_rows[c, g][:].rearrange("p s (j i) -> p j s i", i=4))

        def store_planes(c, g):
            codes = passing("codes", [P, GROUP], U32, 4)
            scale_bytes = passing("scale_bytes", [P, GROUP], U8, 4)
            quantise(codes, scale_bytes, out_bf16[c, g])
            cols = slice(GROUP * g, GROUP * (g + 1))
            nc.sync.dma_start(
                out=out_1[c, :, cols, :].rearrange("p r s -> p (r s)").bitcast(I32), in_=codes[:].bitcast(I32)
            )
            queue = nc.scalar if c == N_CHUNKS - 1 else nc.sync
            for Q in range(4):
                queue.dma_start(
                    out=out_2[c, 4 * Q : 4 * Q + 4, cols].bitcast(I32), in_=scale_bytes[32 * Q : 32 * Q + 4, :].bitcast(I32)
                )

        turn_q(0, 0)
        turn_q(0, 1)
        order_words(0)
        order_words(1)
        make_x(0, 0)
        turn_qe(0, 0)
        turn_q(1, 0)
        make_x(0, 1)
        order_scales(0)
        start_b(0, 0)
        turn_q(1, 1)
        start_b(0, 1)
        quantise_x(0, 0)
        quantise_x(0, 1)
        order_scales(1)
        make_x(1, 0)
        add_qe(0, 0)
        start_b(1, 0)
        multiply_x(0, 0)
        finish_b(0, 0)
        start_b(1, 1)
        make_x(1, 1)
        turn_qe(1, 0)
        add_qe(1, 0)
        turn_qe(0, 1)
        scale_b(0, 0)
        add_qe(0, 1)
        multiply_x(0, 1)
        turn_qe(1, 1)
        finish_b(0, 1)
        pack_be(0, 0)
        quantise_x(1, 0)
        quantise_be(0, 0)
        quantise_x(1, 1)
        multiply_x(1, 1)
        add_qe(1, 1)
        add_qe_on_gpsimd(1, 0)
        finish_b(1, 1)
        scale_b(0, 1)
        multiply_x(1, 0)
        pack_be(0, 1)
        quantise_be(0, 1)
        finish_b(1, 0)
        multiply_be(0, 0)
        scale_b(1, 1)
        scale_b(1, 0)
        finish_out(0, 0)
        pack_be(1, 1)
        pack_be(1, 0)
        multiply_be(0, 1)
        finish_out(0, 1)
        quantise_be(1, 1)
        quantise_be(1, 0)
        turn_out(0, 0)
        empty_out(0, 0)
        turn_out(0, 1)
        empty_out(0, 1)
        multiply_be(1, 0)
        finish_out(1, 0)
        multiply_be(1, 1)
        round_out(0, 0)
        finish_out(1, 1)
        turn_out(1, 0)
        empty_out(1, 0)
        round_out(0, 1)
        turn_out(1, 1)
        empty_out(1, 1)
        store_planes(0, 1)
        round_out(1, 1)
        store_planes(0, 0)
        round_out(1, 0)
        store_planes(1, 0)
        store_planes(1, 1)
